import numpy as np
import ml_dtypes


def mxq(x, axis, fmt="e4m3"):
    dtype, down = {"e4m3": (ml_dtypes.float8_e4m3fn, 7), "e5m2": (ml_dtypes.float8_e5m2, 14)}[fmt]
    v = np.moveaxis(np.asarray(x, np.float32).astype(ml_dtypes.bfloat16).astype(np.float64), axis, -1)
    blocks = v.reshape(v.shape[:-1] + (-1, 32))
    amax = np.abs(blocks).max(-1, keepdims=True)
    byte = np.maximum(np.where(amax > 0, np.frexp(amax)[1] - 1 + 127, 0) - down, 1)
    scale = np.exp2(byte - 127.0)
    codes = (blocks / scale).astype(np.float32).astype(dtype).astype(np.float64)
    return np.moveaxis((codes * scale).reshape(v.shape), -1, axis)


WIDE = False


def mx_kscale(k):
    if not WIDE:
        return np.ones(k)
    levels = np.array([10, -10, 5, -5, 0])
    if k % 512:
        return np.exp2(np.random.permutation(np.resize(levels, k // 32))).repeat(32)
    a = np.empty((k // 512, 16))
    for p in range(k // 512):
        a[p, :8] = np.random.permutation(np.resize(levels, 8))
        for g in range(8):
            far = levels[np.abs(levels - a[p, g]) >= 10]
            a[p, g + 8] = far[np.random.randint(len(far))]
    return np.exp2(a.ravel()).repeat(32)


BF16 = ml_dtypes.bfloat16


def bf(x):
    return np.asarray(x, np.float32).astype(BF16)


def f64(x):
    return np.asarray(x).astype(np.float64)


E2M1 = np.array([0.0, 0.5, 1.0, 1.5, 2.0, 3.0, 4.0, 6.0, -0.0, -0.5, -1.0, -1.5, -2.0, -3.0, -4.0, -6.0])


def pack_weight(w, fmt):
    k, n = w.shape
    w = f64(bf(w)).reshape(k // 32, 32, n)
    amax = np.abs(w).max(1)
    if fmt == "e4m3":
        byte = np.frexp(amax)[1] - 1 + 127 - 7
    else:
        mant, ex = np.frexp(amax / 6.0)
        byte = np.where(mant > 0.5, ex, ex - 1) + 127
    byte = np.clip(np.where(amax > 0, byte, 1), 1, 254)
    scaled = (w * np.exp2(127.0 - byte)[:, None, :]).reshape(k, n).astype(np.float32)
    by_word = np.ascontiguousarray(scaled.reshape(k // 512, 128, 4, n).transpose(0, 1, 3, 2))
    if fmt == "e4m3":
        words = by_word.astype(ml_dtypes.float8_e4m3fn).view(np.uint8)
    else:
        c = by_word.astype(ml_dtypes.float4_e2m1fn).view(np.uint8) & 0xF
        words = c[..., 0::2] | (c[..., 1::2] << 4)
    return np.ascontiguousarray(words), np.ascontiguousarray(byte.astype(np.uint8).reshape(k // 512, 16, n))


def unpack_weight(words, scales, fmt):
    g, p, n, _ = words.shape
    if fmt == "e4m3":
        vals = np.ascontiguousarray(words).view(ml_dtypes.float8_e4m3fn).astype(np.float64)
    else:
        nib = np.empty((g, p, n, 4), np.uint8)
        nib[..., 0::2] = words & 0xF
        nib[..., 1::2] = words >> 4
        vals = E2M1[nib]
    vals = vals * np.repeat(np.exp2(scales.astype(np.float64) - 127.0), 8, axis=1)[..., None]
    return vals.transpose(0, 1, 3, 2).reshape(g * 512, n)
def pack4(w):
    words, scales = pack_weight(w, "e2m1")
    return words.reshape(words.shape[0], 128, -1), scales


def unpack4(words, scales):
    return unpack_weight(words.reshape(words.shape[0], 128, -1, 2), scales, "e2m1")


E4M3FN = np.array([(-1.0 if i & 128 else 1.0) * ((1.0 + (i & 7) / 8.0) * 2.0 ** (((i >> 3) & 15) - 7) if i & 120 else (i & 7) * 2.0 ** -9) for i in range(256)])


def e4m3fn_bytes(y):
    return np.clip(np.asarray(y, np.float64), -448.0, 448.0).astype(np.float32).astype(ml_dtypes.float8_e4m3fn).view(np.uint8)


def e4m3fn_values(b):
    return E4M3FN[b]

def planes(Y):
    n, m = Y.shape
    b = f64(bf(Y)).reshape(n // 32, 32, m)
    amax = np.abs(b).max(1)
    byte = np.clip(np.where(amax > 0, np.frexp(amax)[1] - 1 + 127 - 7, 1), 1, 254)
    codes = (b * np.exp2(127.0 - byte)[:, None, :]).reshape(n, m).astype(np.float32).astype(ml_dtypes.float8_e4m3fn).view(np.uint8)
    words = codes.reshape(n // 512, 128, 4, m).transpose(0, 1, 3, 2)
    return np.ascontiguousarray(words), np.ascontiguousarray(byte.astype(np.uint8).reshape(n // 512, 16, m))


T, K, N, B = 1024, 2048, 1024, 128


def setup_inputs():
    s = mx_kscale(K)[:, None]
    x_words, x_scales = pack_weight(np.random.randn(K, T) * s, "e4m3")
    size = np.exp(0.4 * np.random.randn(K // B, N // B))
    U = np.random.randn(K, N) / np.sqrt(K) / s * np.repeat(np.repeat(size, B, axis=0), B, axis=1)
    U_scale = (np.abs(U).reshape(K // B, B, N // B, B).max(axis=(1, 3)) / 448.0).astype(np.float32)
    U_bytes = e4m3fn_bytes(U / np.repeat(np.repeat(f64(U_scale), B, axis=0), B, axis=1))
    R_words, R_scales = pack4(np.random.randn(K, N) / np.sqrt(K) / s)
    return {
        "x_words": x_words, "x_scales": x_scales,
        "U_bytes": U_bytes, "U_scale": U_scale,
        "R_words": R_words, "R_scales": R_scales,
        "u_bias": bf(0.4 * np.random.randn(1, N)),
        "r_bias": bf(0.4 * np.random.randn(1, N)),
        "feat_weight": bf(np.exp(0.8 * np.random.randn(1, N))),
    }

def reference(x_words, x_scales, U_bytes, U_scale, R_words, R_scales, u_bias, r_bias, feat_weight):
    X = unpack_weight(x_words, x_scales, "e4m3")
    U = e4m3fn_values(U_bytes) * np.repeat(np.repeat(f64(U_scale), B, axis=0), B, axis=1)
    R = unpack4(R_words, R_scales)
    pred = (X.T @ mxq(U, 0, "e4m3")) + f64(u_bias)
    target = np.tanh((X.T @ R) + f64(r_bias))
    diff = pred - target
    y = diff * diff * f64(feat_weight)
    Y = y.T
    words, scales = planes(Y)
    return y, words, scales

@@ -1,0 +1,408 @@
+from contextlib import ExitStack
+
+import concourse.mybir as mybir
+from concourse.masks import make_identity
+
+T, K, N = 1024, 2048, 1024
+FLOPS = 2 * 2 * T * K * N
+
+F32 = mybir.dt.float32
+BF16 = mybir.dt.bfloat16
+I32 = mybir.dt.int32
+U32 = mybir.dt.uint32
+U8 = mybir.dt.uint8
+FP8 = mybir.dt.float8_e4m3fn
+FP8X4 = mybir.dt.float8_e4m3fn_x4
+FP4X4 = mybir.dt.float4_e2m1fn_x4
+ACT = mybir.ActivationFunctionType
+ALU = mybir.AluOpType
+
+P = 128
+PACK = 4
+PASSES = K // (P * PACK)
+HALF = 512
+TILES = HALF // P
+LEAD = 8
+RUN = 4
+PIECES_PER_STEP = 3
+SCALAR_TILE = 3
+SCALAR_ROWS = 2
+EARLY_TANH = 2
+WIDEN_IDLE = 4
+WIDEN_PER_STEP = 3
+SCALAR_ROUND_FROM = 2
+
+
+def tile_distillation_curiosity_terms_b7_kernel(
+    tc, x_words, x_scales, U_bytes, U_scale, R_words, R_scales, u_bias, r_bias, feat_weight, out_0, out_1, out_2
+):
+    nc = tc.nc
+    with ExitStack() as ctx:
+        keep = ctx.enter_context(tc.tile_pool(name="keep", bufs=1))
+        work = ctx.enter_context(tc.tile_pool(name="work", bufs=2))
+        psum = ctx.enter_context(tc.psum_pool(name="psum", bufs=8))
+        ctx.enter_context(tc.manual_schedule())
+
+        x_plane = keep.tile([P, PASSES, T], U8, name="x_plane", align_bytes=64)
+        r_plane = keep.tile([P, PASSES, N], U8, name="r_plane", align_bytes=64)
+        nc.vector.memset(x_plane[:].rearrange("p g n -> p (g n)").bitcast(I32), 0)
+        nc.vector.memset(r_plane[:].rearrange("p g n -> p (g n)").bitcast(I32), 0)
+
+        ident = keep.tile([P, P], F32, name="ident")
+        scale_all = keep.tile([P, 16, 8], F32, name="scale_all")
+        vec_rows = keep.tile([P, P], BF16, name="vec_rows")
+
+        warm = keep.tile([P, 1], F32, name="warm")
+        nc.vector.memset(warm[:], 0.0)
+        warm_out = keep.tile([P, 1], F32, name="warm_out")
+        nc.scalar.activation(out=warm_out[:], in_=warm[:], func=ACT.Tanh)
+
+        u_raw, x_code, r_code = {}, {}, {}
+        x_rows = x_words.rearrange("g p n t -> p g (n t)")
+        r_rows = R_words.rearrange("g p b -> p g b")
+
+        def load_u(c):
+            u_raw[c] = keep.tile([P, PACK, N], U8, name="u_raw_%d" % c)
+            rows = U_bytes[c * 512 : (c + 1) * 512, :]
+            nc.sync.dma_start(out=u_raw[c][:], in_=rows.rearrange("(p t) n -> p t n", t=PACK))
+
+        def load_x(h, c0, c1):
+            words = keep.tile([P, c1 - c0, HALF], U32, name="x_code_%d_%d" % (h, c0), align_bytes=64)
+            nc.sync.dma_start(
+                out=words[:].bitcast(I32), in_=x_rows[:, c0:c1, h * HALF * 4 : (h + 1) * HALF * 4].bitcast(I32)
+            )
+            for c in range(c0, c1):
+                x_code[h, c] = words[:, c - c0, :]
+
+        def load_r(g, c0, c1):
+            words = keep.tile([P, c1 - c0, 2 * HALF], U8, name="r_code_%d_%d" % (g, c0), align_bytes=64)
+            nc.sync.dma_start(
+                out=words[:].bitcast(I32), in_=r_rows[:, c0:c1, g * HALF * 2 : (g + 1) * HALF * 2].bitcast(I32)
+            )
+            for c in range(c0, c1):
+                r_code[g, c] = words[:, c - c0, :]
+
+        def load_plane(queue, plane, scales, q):
+            queue.dma_start(
+                out=plane[32 * q : 32 * q + 4, :, :].bitcast(I32),
+                in_=scales[:, 4 * q : 4 * q + 4, :].rearrange("g r n -> r g n").bitcast(I32),
+            )
+
+        load_u(0)
+        load_x(0, 0, 1)
+        load_r(0, 0, 2)
+        for q in range(4):
+            load_plane(nc.sync, x_plane, x_scales, q)
+        nc.gpsimd.memset(vec_rows[:], 0.0)
+        for q in range(4):
+            load_plane(nc.sync if q < 2 else nc.gpsimd, r_plane, R_scales, q)
+        nc.gpsimd.dma_start(
+            out=scale_all[:].rearrange("p i j -> p (i j)"),
+            in_=U_scale.rearrange("i j -> (i j)").partition_broadcast(P),
+        )
+        for i, vec in enumerate((r_bias, u_bias, feat_weight)):
+            nc.gpsimd.dma_start(out=vec_rows[8 * i : 8 * i + 8, :], in_=vec.rearrange("o (j p) -> (o j) p", p=P))
+        make_identity(nc, ident[:])
+        load_x(0, 1, 2)
+        load_x(0, 2, 3)
+        load_r(0, 2, 4)
+        load_x(0, 3, 4)
+        load_u(1)
+        load_r(1, 0, 4)
+        load_u(2)
+        load_u(3)
+        load_x(1, 0, 2)
+        load_x(1, 2, 4)
+
+        u_wide, u_grp, u_code, u_plane = {}, {}, {}, {}
+        scale_col = keep.tile([P, PASSES, 8], F32, name="scale_col")
+        vec_col = keep.tile([P, 24], F32, name="vec_col")
+
+        def pick_scales():
+            by_quadrant = scale_all[:].rearrange("p (c q) j -> p q c j", q=4)
+            for q in range(4):
+                rows = slice(32 * q, 32 * q + 32)
+                nc.vector.tensor_copy(out=scale_col[rows, :, :], in_=by_quadrant[rows, q, :, :])
+
+        def widen(g, c, t, on_scalar):
+            if (g, c) not in u_wide:
+                u_wide[g, c] = keep.tile([P, PACK, HALF], BF16, name="u_wide_%d_%d" % (g, c))
+            src = u_raw[c][:, t, g * HALF : (g + 1) * HALF].bitcast(FP8)
+            if on_scalar:
+                nc.scalar.copy(out=u_wide[g, c][:, t, :], in_=src)
+            else:
+                nc.vector.tensor_copy(out=u_wide[g, c][:, t, :], in_=src)
+
+        def interleave(g, j, c, on_scalar):
+            if (g, j) not in u_grp:
+                u_grp[g, j] = work.tile([P, PASSES, P, PACK], BF16, name="u_grp", bufs=6, align_bytes=64)
+            src = u_wide[g, c][:, :, j * P : (j + 1) * P].rearrange("p t (a i) -> p a t i", i=RUN)
+            dst = u_grp[g, j][:, c, :, :].rearrange("p (a i) t -> p a t i", i=RUN)
+            col = scale_col[:, c, g * TILES + j : g * TILES + j + 1]
+            if on_scalar:
+                nc.scalar.activation(out=dst, in_=src, func=ACT.Copy, scale=col)
+            else:
+                nc.vector.tensor_scalar(out=dst, in0=src, scalar1=col, scalar2=None, op0=ALU.mult)
+
+        def quantize_u(g, j):
+            u_code[g, j] = keep.tile([P, PASSES, P], U32, name="u_code_%d_%d" % (g, j), align_bytes=64)
+            u_plane[g, j] = keep.tile([P, PASSES, P], U8, name="u_plane_%d_%d" % (g, j), align_bytes=64)
+            nc.vector.quantize_mx(
+                out=u_code[g, j][:].rearrange("p c n -> p (c n)").bitcast(FP8X4),
+                scales=u_plane[g, j][:].rearrange("p c n -> p (c n)"),
+                in_=u_grp[g, j][:].rearrange("p c n t -> p (c n t)"),
+            )
+
+        target, diff, y_feat, y_tok, y_pairs, y_grp, turned, pred = {}, {}, {}, {}, {}, {}, {}, {}
+        y_plane = keep.tile([P, 2, T], U8, name="y_plane", align_bytes=64)
+
+        def mx_pass(acc, h, c, weights, plane):
+            nc.tensor.matmul_mx(
+                out=acc[:],
+                lhsT=weights,
+                lhsT_scale=plane,
+                rhs=x_code[h, c].bitcast(FP8X4),
+                rhs_scale=x_plane[:, c, h * HALF : (h + 1) * HALF],
+                start=(c == 0),
+                stop=(c == PASSES - 1),
+            )
+
+        def column(which, g, j):
+            i = 8 * which + g * TILES + j
+            return vec_col[:, i : i + 1]
+
+        def r_pass(unit, acc, c):
+            g, j, h = unit
+            n0 = g * HALF + j * P
+            mx_pass(acc, h, c, r_code[g, c][:, 2 * j * P : 2 * (j + 1) * P].bitcast(FP4X4), r_plane[:, c, n0 : n0 + P])
+
+        def r_product(unit):
+            acc = psum.tile([P, HALF], F32, name="bank")
+            for c in range(PASSES):
+                r_pass(unit, acc, c)
+            return acc
+
+        def r_tanh(unit, acc):
+            g, j, h = unit
+            target[unit] = work.tile([P, HALF], F32, name="target", bufs=12)
+            nc.scalar.activation(out=target[unit][:], in_=acc[:], func=ACT.Tanh, bias=column(0, g, j))
+
+        def u_product(unit):
+            g, j, h = unit
+            pred[unit] = psum.tile([P, HALF], F32, name="bank")
+            for c in range(PASSES):
+                mx_pass(pred[unit], h, c, u_code[g, j][:, c, :].bitcast(FP8X4), u_plane[g, j][:, c, :])
+
+        def subtract(unit):
+            g, j, h = unit
+            diff[unit] = work.tile([P, HALF], F32, name="diff", bufs=2)
+            nc.vector.scalar_tensor_tensor(
+                out=diff[unit][:], in0=pred[unit][:], scalar=column(1, g, j), in1=target[unit][:],
+                op0=ALU.add, op1=ALU.subtract,
+            )
+
+        def weigh(unit):
+            g, j, h = unit
+            y_feat[unit] = work.tile([P, HALF], F32, name="y_feat", bufs=5)
+            nc.vector.scalar_tensor_tensor(
+                out=y_feat[unit][:], in0=diff[unit][:], scalar=column(2, g, j), in1=diff[unit][:],
+                op0=ALU.mult, op1=ALU.mult,
+            )
+
+        def turn_y(unit):
+            turned[unit] = psum.tile([P, TILES, P], F32, name="bank")
+            for b in range(TILES):
+                nc.tensor.transpose(turned[unit][:, b, :], y_feat[unit][:, b * P : (b + 1) * P], ident[:])
+
+        def copy_y(unit):
+            g, j, h = unit
+            if (g, h) not in y_tok:
+                y_tok[g, h] = work.tile([P, TILES, HALF], F32, name="y_tok", bufs=3)
+            nc.scalar.copy(out=y_tok[g, h][:, :, j * P : (j + 1) * P], in_=turned[unit][:])
+
+        def store_y(g, h, j0, j1):
+            rows = out_0[h * HALF : (h + 1) * HALF, g * HALF + j0 * P : g * HALF + j1 * P]
+            nc.sync.dma_start(out=rows.rearrange("(b p) n -> p b n", p=P), in_=y_tok[g, h][:, :, j0 * P : j1 * P])
+
+        def round_y(unit, on_scalar, from_bank):
+            g, j, h = unit
+            if (g, h) not in y_pairs:
+                y_pairs[g, h] = work.tile([P, TILES, 2, P, 2], BF16, name="y_pairs", bufs=2)
+            dst = y_pairs[g, h][:, :, :, 32 * j : 32 * j + 32, :]
+            src = turned[unit][:] if from_bank else y_tok[g, h][:, :, j * P : (j + 1) * P]
+            src = src.rearrange("p b (q u e) -> p b u q e", u=2, e=2)
+            if on_scalar:
+                nc.scalar.copy(out=dst, in_=src)
+            else:
+                nc.vector.tensor_copy(out=dst, in_=src)
+
+        def turn_pairs(g, h):
+            words = y_pairs[g, h][:].rearrange("p b u q e -> p (b u q e)").bitcast(F32)
+            for i in range(2):
+                bank = psum.tile([P, 2, 2, P], F32, name="bank")
+                turned[g, h, i, "pairs"] = bank
+                for b in range(2):
+                    for u in range(2):
+                        w0 = ((2 * i + b) * 2 + u) * P
+                        nc.tensor.transpose(bank[:, b, u, :], words[:, w0 : w0 + P], ident[:])
+
+        def copy_pairs(g, h, i, on_scalar):
+            if (g, h) not in y_grp:
+                y_grp[g, h] = work.tile([P, HALF * PACK], BF16, name="y_grp", bufs=2, align_bytes=64)
+            words = y_grp[g, h][:].bitcast(F32).rearrange("p (i b r u) -> p i b r u", i=2, b=2, u=2)
+            src = turned[g, h, i, "pairs"][:].rearrange("p b u r -> p b r u")
+            if on_scalar:
+                nc.scalar.copy(out=words[:, i, :, :, :], in_=src)
+            else:
+                nc.vector.tensor_copy(out=words[:, i, :, :, :], in_=src)
+
+        def quantize_y(g, h):
+            codes = work.tile([P, HALF], U32, name="y_code", bufs=2, align_bytes=64)
+            nc.vector.quantize_mx(
+                out=codes[:].bitcast(FP8X4), scales=y_plane[:, g, h * HALF : (h + 1) * HALF], in_=y_grp[g, h][:]
+            )
+            dst = out_1[g].rearrange("p m t -> p (m t)")[:, h * HALF * 4 : (h + 1) * HALF * 4]
+            nc.sync.dma_start(out=dst.bitcast(I32), in_=codes[:].bitcast(I32))
+
+        def store_plane(g):
+            for q in range(4):
+                nc.sync.dma_start(
+                    out=out_2[g, 4 * q : 4 * q + 4, :].bitcast(I32), in_=y_plane[32 * q : 32 * q + 4, g, :].bitcast(I32)
+                )
+
+        r_units = [(g, j, h) for h in range(2) for g in range(2) for j in range(TILES)]
+        u_units = [(g, j, h) for g in range(2) for h in range(2) for j in range(TILES)]
+        steps = len(u_units)
+        late_rows = [(c, t) for c in range(PASSES) for t in range(PACK)]
+
+        def widen_late(count):
+            for c, t in late_rows[:count]:
+                widen(1, c, t, True)
+                late_rows.remove((c, t))
+
+        first = []
+        for i in range(TILES):
+            acc = psum.tile([P, HALF], F32, name="bank")
+            first.append(acc)
+        for c in range(PASSES):
+            for i in range(TILES):
+                r_pass(r_units[i], first[i], c)
+
+        def widen_first(c):
+            for t in range(PACK):
+                widen(0, c, t, t >= PACK - SCALAR_ROWS)
+
+        widen_first(0)
+        widen_late(WIDEN_IDLE)
+        pick_scales()
+        for j in range(TILES):
+            interleave(0, j, 0, False)
+        vec_wide = keep.tile([P, P], F32, name="vec_wide")
+        nc.vector.tensor_copy(out=vec_wide[:], in_=vec_rows[:])
+        widen_first(1)
+        vec_turn = psum.tile([P, TILES, P], F32, name="bank")
+        nc.tensor.transpose(vec_turn[:, 0, :], vec_wide[:], ident[:])
+        nc.scalar.copy(out=vec_col[:], in_=vec_turn[:, 0, 0:24])
+        for i in range(EARLY_TANH):
+            r_tanh(r_units[i], first[i])
+        for i in range(TILES, LEAD):
+            first.append(r_product(r_units[i]))
+        for j in range(TILES):
+            interleave(0, j, 1, False)
+        widen_first(2)
+        interleave(0, 0, 2, False)
+        widen_first(3)
+        interleave(0, 1, 2, False)
+        interleave(0, 0, 3, False)
+        interleave(0, 1, 3, False)
+        quantize_u(0, 0)
+        for i in range(EARLY_TANH, LEAD):
+            r_tanh(r_units[i], first[i])
+
+        pieces = [("i", 0, 2, 2), ("q", 0, 1, 0), ("i", 0, 2, 3), ("i", 0, 3, 2), ("q", 0, 2, 0)]
+        pieces = pieces + [("i", 0, 3, 3), ("i", 1, 0, 0), ("q", 0, 3, 0)]
+        pieces = pieces + [("i", 1, j, c) for c in range(PASSES - 1) for j in range(TILES)][1:]
+        for j in range(TILES):
+            pieces.append(("i", 1, j, PASSES - 1))
+            if j > 0:
+                pieces.append(("q", 1, j - 1, 0))
+        pieces.append(("q", 1, TILES - 1, 0))
+
+        def prepare(count):
+            for piece in pieces[:count]:
+                kind, g, j, c = piece
+                if kind == "i":
+                    interleave(g, j, c, g == 1 and j >= SCALAR_TILE and c < PASSES - 1)
+                else:
+                    quantize_u(g, j)
+                pieces.remove(piece)
+
+        groups = [(g, h) for g in range(2) for h in range(2)]
+        prepare(2)
+        for s in range(steps - 2):
+            unit = u_units[s]
+            u_product(unit)
+            subtract(unit)
+            if s >= 4 and s % 2 == 0:
+                round_y(u_units[s - 4], False, False)
+            elif s >= 9 and s % 4 == 1:
+                quantize_y(*groups[s // 4 - 2])
+            else:
+                prepare(1)
+            weigh(unit)
+            if 4 <= s <= SCALAR_ROUND_FROM and s % 2 == 0:
+                round_y(u_units[s - 3], False, False)
+            if s == 13:
+                store_plane(0)
+            if s + LEAD < steps:
+                r_tanh(r_units[s + LEAD], r_product(r_units[s + LEAD]))
+            widen_late(WIDEN_PER_STEP)
+            prepare(PIECES_PER_STEP)
+            if s >= 3 and s % 2 == 1:
+                turn_y(u_units[s - 3])
+                turn_y(u_units[s - 2])
+                if s >= 7 and s % 4 == 3:
+                    turn_pairs(*groups[s // 4 - 1])
+                copy_y(u_units[s - 3])
+                copy_y(u_units[s - 2])
+                if s >= SCALAR_ROUND_FROM:
+                    round_y(u_units[s - 2], True, True)
+                if s >= 7 and s % 4 == 3:
+                    for i in range(2):
+                        copy_pairs(*groups[s // 4 - 1], i, True)
+                if s % 4 == 1:
+                    g, h = groups[s // 4 - 1]
+                    store_y(g, h, 0, TILES)
+
+        last = u_units[12:]
+        u_product(last[2])
+        subtract(last[2])
+        round_y(u_units[10], False, False)
+        weigh(last[2])
+        turn_y(last[0])
+        turn_y(last[1])
+        copy_y(last[0])
+        copy_y(last[1])
+        store_y(1, 1, 0, 2)
+        u_product(last[3])
+        subtract(last[3])
+        round_y(last[0], False, False)
+        weigh(last[3])
+        turn_pairs(1, 0)
+        turn_y(last[2])
+        round_y(last[1], False, False)
+        copy_y(last[2])
+        store_y(1, 1, 2, 3)
+        round_y(last[2], False, False)
+        turn_y(last[3])
+        copy_pairs(1, 0, 0, True)
+        round_y(last[3], False, True)
+        copy_pairs(1, 0, 1, True)
+        copy_y(last[3])
+        store_y(1, 1, 3, 4)
+        turn_pairs(1, 1)
+        quantize_y(1, 0)
+        copy_pairs(1, 1, 0, False)
+        copy_pairs(1, 1, 1, True)
+        quantize_y(1, 1)
+        store_plane(1)

@@ -22,15 +22,19 @@ PACK = 4
 PASSES = K // (P * PACK)
 HALF = 512
 TILES = HALF // P
-LEAD = 8
+LEAD = 12
 RUN = 4
-PIECES_PER_STEP = 3
-SCALAR_TILE = 3
-SCALAR_ROWS = 2
-EARLY_TANH = 2
-WIDEN_IDLE = 4
-WIDEN_PER_STEP = 3
+ORDER = "x1 x2 r0 x3 v r1 u1 r2 u2 y0 u3 y1"
+U_FIRST = 1
+V_ROWS = (3, 3, 2, 2)
+V_RATE = 2
+S_RATE = 2
+S_BLOCKS = 0
 SCALAR_ROUND_FROM = 2
+TANH_AT = (4, 4, 4, 4)
+BOTH_FROM = 2
+TAIL = 0
+WIDE_FIRST = 1
 
 
 def tile_distillation_curiosity_terms_b7_kernel(
@@ -49,7 +53,7 @@ def tile_distillation_curiosity_terms_b7_kernel(
         nc.vector.memset(r_plane[:].rearrange("p g n -> p (g n)").bitcast(I32), 0)
 
         ident = keep.tile([P, P], F32, name="ident")
-        scale_all = keep.tile([P, 16, 8], F32, name="scale_all")
+        scale_flat = keep.tile([P, 1], F32, name="scale_flat")
         vec_rows = keep.tile([P, P], BF16, name="vec_rows")
 
         warm = keep.tile([P, 1], F32, name="warm")
@@ -88,38 +92,42 @@ def tile_distillation_curiosity_terms_b7_kernel(
                 in_=scales[:, 4 * q : 4 * q + 4, :].rearrange("g r n -> r g n").bitcast(I32),
             )
 
-        load_u(0)
+        nc.gpsimd.dma_start(out=scale_flat[:], in_=U_scale.rearrange("i (j o) -> (i j) o", o=1))
+        make_identity(nc, ident[:])
+        nc.gpsimd.memset(vec_rows[:], 0.0)
         load_x(0, 0, 1)
         load_r(0, 0, 2)
-        for q in range(4):
+        load_plane(nc.sync, x_plane, x_scales, 0)
+        if U_FIRST:
+            load_u(0)
+        for q in range(1, 4):
             load_plane(nc.sync, x_plane, x_scales, q)
-        nc.gpsimd.memset(vec_rows[:], 0.0)
         for q in range(4):
-            load_plane(nc.sync if q < 2 else nc.gpsimd, r_plane, R_scales, q)
-        nc.gpsimd.dma_start(
-            out=scale_all[:].rearrange("p i j -> p (i j)"),
-            in_=U_scale.rearrange("i j -> (i j)").partition_broadcast(P),
-        )
-        for i, vec in enumerate((r_bias, u_bias, feat_weight)):
-            nc.gpsimd.dma_start(out=vec_rows[8 * i : 8 * i + 8, :], in_=vec.rearrange("o (j p) -> (o j) p", p=P))
-        make_identity(nc, ident[:])
-        load_x(0, 1, 2)
-        load_x(0, 2, 3)
-        load_r(0, 2, 4)
-        load_x(0, 3, 4)
-        load_u(1)
-        load_r(1, 0, 4)
-        load_u(2)
-        load_u(3)
-        load_x(1, 0, 2)
-        load_x(1, 2, 4)
+            load_plane(nc.sync, r_plane, R_scales, q)
+        for item in ORDER.split():
+            if item == "v":
+                for i, vec in enumerate((r_bias, u_bias, feat_weight)):
+                    nc.sync.dma_start(out=vec_rows[8 * i : 8 * i + 8, :], in_=vec.rearrange("o (j p) -> (o j) p", p=P))
+            elif item[0] == "u":
+                load_u(int(item[1]))
+            elif item[0] == "x":
+                load_x(0, int(item[1]), int(item[1]) + 1)
+            elif item[0] == "y":
+                load_x(1, 2 * int(item[1]), 2 * int(item[1]) + 2)
+            elif item == "r0":
+                load_r(0, 2, 4)
+            elif item == "r1":
+                load_r(1, 0, 2)
+            else:
+                load_r(1, 2, 4)
 
         u_wide, u_grp, u_code, u_plane = {}, {}, {}, {}
         scale_col = keep.tile([P, PASSES, 8], F32, name="scale_col")
         vec_col = keep.tile([P, 24], F32, name="vec_col")
 
         def pick_scales():
-            by_quadrant = scale_all[:].rearrange("p (c q) j -> p q c j", q=4)
+            nc.tensor.transpose(spread[:, 0, :], scale_flat[:].to_broadcast([P, P]), ident[:])
+            by_quadrant = spread[:, 0, :].rearrange("p (c q j) -> p q c j", q=4, j=8)
             for q in range(4):
                 rows = slice(32 * q, 32 * q + 32)
                 nc.vector.tensor_copy(out=scale_col[rows, :, :], in_=by_quadrant[rows, q, :, :])
@@ -133,36 +141,37 @@ def tile_distillation_curiosity_terms_b7_kernel(
             else:
                 nc.vector.tensor_copy(out=u_wide[g, c][:, t, :], in_=src)
 
-        def interleave(g, j, c, on_scalar):
-            if (g, j) not in u_grp:
-                u_grp[g, j] = work.tile([P, PASSES, P, PACK], BF16, name="u_grp", bufs=6, align_bytes=64)
+        def interleave(g, c, j, on_scalar):
+            if (g, c) not in u_grp:
+                u_grp[g, c] = work.tile([P, TILES, P, PACK], BF16, name="u_grp", bufs=3, align_bytes=64)
             src = u_wide[g, c][:, :, j * P : (j + 1) * P].rearrange("p t (a i) -> p a t i", i=RUN)
-            dst = u_grp[g, j][:, c, :, :].rearrange("p (a i) t -> p a t i", i=RUN)
+            dst = u_grp[g, c][:, j, :, :].rearrange("p (a i) t -> p a t i", i=RUN)
             col = scale_col[:, c, g * TILES + j : g * TILES + j + 1]
             if on_scalar:
                 nc.scalar.activation(out=dst, in_=src, func=ACT.Copy, scale=col)
             else:
                 nc.vector.tensor_scalar(out=dst, in0=src, scalar1=col, scalar2=None, op0=ALU.mult)
 
-        def quantize_u(g, j):
-            u_code[g, j] = keep.tile([P, PASSES, P], U32, name="u_code_%d_%d" % (g, j), align_bytes=64)
-            u_plane[g, j] = keep.tile([P, PASSES, P], U8, name="u_plane_%d_%d" % (g, j), align_bytes=64)
+        def quantize_u(g, c, j0, j1):
+            if (g, c) not in u_code:
+                u_code[g, c] = keep.tile([P, TILES, P], U32, name="u_code_%d_%d" % (g, c), align_bytes=64)
+                u_plane[g, c] = keep.tile([P, TILES, P], U8, name="u_plane_%d_%d" % (g, c), align_bytes=64)
             nc.vector.quantize_mx(
-                out=u_code[g, j][:].rearrange("p c n -> p (c n)").bitcast(FP8X4),
-                scales=u_plane[g, j][:].rearrange("p c n -> p (c n)"),
-                in_=u_grp[g, j][:].rearrange("p c n t -> p (c n t)"),
+                out=u_code[g, c][:, j0:j1, :].rearrange("p j n -> p (j n)").bitcast(FP8X4),
+                scales=u_plane[g, c][:, j0:j1, :].rearrange("p j n -> p (j n)"),
+                in_=u_grp[g, c][:, j0:j1, :, :].rearrange("p j n t -> p (j n t)"),
             )
 
         target, diff, y_feat, y_tok, y_pairs, y_grp, turned, pred = {}, {}, {}, {}, {}, {}, {}, {}
         y_plane = keep.tile([P, 2, T], U8, name="y_plane", align_bytes=64)
 
-        def mx_pass(acc, h, c, weights, plane):
+        def mx_pass(acc, h, c, weights, plane, b0=0, b1=TILES):
             nc.tensor.matmul_mx(
                 out=acc[:],
                 lhsT=weights,
                 lhsT_scale=plane,
-                rhs=x_code[h, c].bitcast(FP8X4),
-                rhs_scale=x_plane[:, c, h * HALF : (h + 1) * HALF],
+                rhs=x_code[h, c][:, b0 * P : b1 * P].bitcast(FP8X4),
+                rhs_scale=x_plane[:, c, h * HALF + b0 * P : h * HALF + b1 * P],
                 start=(c == 0),
                 stop=(c == PASSES - 1),
             )
@@ -187,64 +196,63 @@ def tile_distillation_curiosity_terms_b7_kernel(
             target[unit] = work.tile([P, HALF], F32, name="target", bufs=12)
             nc.scalar.activation(out=target[unit][:], in_=acc[:], func=ACT.Tanh, bias=column(0, g, j))
 
-        def u_product(unit):
+        def u_product(unit, b0=0, b1=TILES):
             g, j, h = unit
-            pred[unit] = psum.tile([P, HALF], F32, name="bank")
+            pred[unit, b0] = psum.tile([P, (b1 - b0) * P], F32, name="bank")
             for c in range(PASSES):
-                mx_pass(pred[unit], h, c, u_code[g, j][:, c, :].bitcast(FP8X4), u_plane[g, j][:, c, :])
+                mx_pass(pred[unit, b0], h, c, u_code[g, c][:, j, :].bitcast(FP8X4), u_plane[g, c][:, j, :], b0, b1)
 
-        def subtract(unit):
+        def subtract(unit, b0=0, b1=TILES):
             g, j, h = unit
-            diff[unit] = work.tile([P, HALF], F32, name="diff", bufs=2)
+            diff[unit, b0] = work.tile([P, (b1 - b0) * P], F32, name="diff", bufs=2)
             nc.vector.scalar_tensor_tensor(
-                out=diff[unit][:], in0=pred[unit][:], scalar=column(1, g, j), in1=target[unit][:],
-                op0=ALU.add, op1=ALU.subtract,
+                out=diff[unit, b0][:], in0=pred[unit, b0][:], scalar=column(1, g, j),
+                in1=target[unit][:, b0 * P : b1 * P], op0=ALU.add, op1=ALU.subtract,
             )
 
-        def weigh(unit):
+        def weigh(unit, b0=0, b1=TILES):
             g, j, h = unit
-            y_feat[unit] = work.tile([P, HALF], F32, name="y_feat", bufs=5)
+            y_feat[unit, b0] = work.tile([P, (b1 - b0) * P], F32, name="y_feat", bufs=5)
             nc.vector.scalar_tensor_tensor(
-                out=y_feat[unit][:], in0=diff[unit][:], scalar=column(2, g, j), in1=diff[unit][:],
+                out=y_feat[unit, b0][:], in0=diff[unit, b0][:], scalar=column(2, g, j), in1=diff[unit, b0][:],
                 op0=ALU.mult, op1=ALU.mult,
             )
 
-        def turn_y(unit):
-            turned[unit] = psum.tile([P, TILES, P], F32, name="bank")
-            for b in range(TILES):
-                nc.tensor.transpose(turned[unit][:, b, :], y_feat[unit][:, b * P : (b + 1) * P], ident[:])
+        def turn_y(unit, b0=0, b1=TILES):
+            turned[unit, b0] = psum.tile([P, b1 - b0, P], F32, name="bank")
+            for b in range(b1 - b0):
+                nc.tensor.transpose(turned[unit, b0][:, b, :], y_feat[unit, b0][:, b * P : (b + 1) * P], ident[:])
 
-        def copy_y(unit):
+        def copy_y(unit, b0=0, b1=TILES):
             g, j, h = unit
             if (g, h) not in y_tok:
                 y_tok[g, h] = work.tile([P, TILES, HALF], F32, name="y_tok", bufs=3)
-            nc.scalar.copy(out=y_tok[g, h][:, :, j * P : (j + 1) * P], in_=turned[unit][:])
+            nc.scalar.copy(out=y_tok[g, h][:, b0:b1, j * P : (j + 1) * P], in_=turned[unit, b0][:])
 
         def store_y(g, h, j0, j1):
             rows = out_0[h * HALF : (h + 1) * HALF, g * HALF + j0 * P : g * HALF + j1 * P]
             nc.sync.dma_start(out=rows.rearrange("(b p) n -> p b n", p=P), in_=y_tok[g, h][:, :, j0 * P : j1 * P])
 
-        def round_y(unit, on_scalar, from_bank):
+        def round_y(unit, on_scalar, from_bank, b0=0, b1=TILES):
             g, j, h = unit
             if (g, h) not in y_pairs:
                 y_pairs[g, h] = work.tile([P, TILES, 2, P, 2], BF16, name="y_pairs", bufs=2)
-            dst = y_pairs[g, h][:, :, :, 32 * j : 32 * j + 32, :]
-            src = turned[unit][:] if from_bank else y_tok[g, h][:, :, j * P : (j + 1) * P]
+            dst = y_pairs[g, h][:, b0:b1, :, 32 * j : 32 * j + 32, :]
+            src = turned[unit, b0][:] if from_bank else y_tok[g, h][:, b0:b1, j * P : (j + 1) * P]
             src = src.rearrange("p b (q u e) -> p b u q e", u=2, e=2)
             if on_scalar:
                 nc.scalar.copy(out=dst, in_=src)
             else:
                 nc.vector.tensor_copy(out=dst, in_=src)
 
-        def turn_pairs(g, h):
-            words = y_pairs[g, h][:].rearrange("p b u q e -> p (b u q e)").bitcast(F32)
-            for i in range(2):
-                bank = psum.tile([P, 2, 2, P], F32, name="bank")
-                turned[g, h, i, "pairs"] = bank
-                for b in range(2):
-                    for u in range(2):
-                        w0 = ((2 * i + b) * 2 + u) * P
-                        nc.tensor.transpose(bank[:, b, u, :], words[:, w0 : w0 + P], ident[:])
+        def turn_pairs(g, h, i):
+            words = y_pairs[g, h][:, 2 * i : 2 * i + 2].rearrange("p b u q e -> p (b u q e)").bitcast(F32)
+            bank = psum.tile([P, 2, 2, P], F32, name="bank")
+            turned[g, h, i, "pairs"] = bank
+            for b in range(2):
+                for u in range(2):
+                    w0 = (b * 2 + u) * P
+                    nc.tensor.transpose(bank[:, b, u, :], words[:, w0 : w0 + P], ident[:])
 
         def copy_pairs(g, h, i, on_scalar):
             if (g, h) not in y_grp:
@@ -256,12 +264,15 @@ def tile_distillation_curiosity_terms_b7_kernel(
             else:
                 nc.vector.tensor_copy(out=words[:, i, :, :, :], in_=src)
 
-        def quantize_y(g, h):
-            codes = work.tile([P, HALF], U32, name="y_code", bufs=2, align_bytes=64)
+        def quantize_y(g, h, b0=0, b1=TILES):
+            codes = work.tile([P, (b1 - b0) * P], U32, name="y_code", bufs=3, align_bytes=64)
+            m0, m1 = h * HALF + b0 * P, h * HALF + b1 * P
             nc.vector.quantize_mx(
-                out=codes[:].bitcast(FP8X4), scales=y_plane[:, g, h * HALF : (h + 1) * HALF], in_=y_grp[g, h][:]
+                out=codes[:].bitcast(FP8X4),
+                scales=y_plane[:, g, m0:m1],
+                in_=y_grp[g, h][:, b0 * P * PACK : b1 * P * PACK],
             )
-            dst = out_1[g].rearrange("p m t -> p (m t)")[:, h * HALF * 4 : (h + 1) * HALF * 4]
+            dst = out_1[g].rearrange("p m t -> p (m t)")[:, m0 * 4 : m1 * 4]
             nc.sync.dma_start(out=dst.bitcast(I32), in_=codes[:].bitcast(I32))
 
         def store_plane(g):
@@ -280,70 +291,98 @@ def tile_distillation_curiosity_terms_b7_kernel(
                 widen(1, c, t, True)
                 late_rows.remove((c, t))
 
-        first = []
-        for i in range(TILES):
-            acc = psum.tile([P, HALF], F32, name="bank")
-            first.append(acc)
-        for c in range(PASSES):
+        def r_four(units):
+            banks = []
             for i in range(TILES):
-                r_pass(r_units[i], first[i], c)
+                acc = psum.tile([P, HALF], F32, name="bank")
+                banks.append(acc)
+            for c in range(PASSES):
+                for i in range(TILES):
+                    r_pass(units[i], banks[i], c)
+            return banks
 
         def widen_first(c):
             for t in range(PACK):
-                widen(0, c, t, t >= PACK - SCALAR_ROWS)
+                widen(0, c, t, t >= V_ROWS[c])
 
-        widen_first(0)
-        widen_late(WIDEN_IDLE)
+        def finish(g, c):
+            for j in range(TILES):
+                interleave(g, c, j, False)
+
+        spread = psum.tile([P, TILES, P], F32, name="bank")
         pick_scales()
-        for j in range(TILES):
-            interleave(0, j, 0, False)
+        first = r_four(r_units[0:4])
+        widen_first(0)
+        widen_late(PACK)
+        finish(0, 0)
+        interleave(1, 0, 0, False)
+        quantize_u(0, 0, 0, TILES)
+        for j in range(1, TILES):
+            interleave(1, 0, j, False)
         vec_wide = keep.tile([P, P], F32, name="vec_wide")
         nc.vector.tensor_copy(out=vec_wide[:], in_=vec_rows[:])
-        widen_first(1)
-        vec_turn = psum.tile([P, TILES, P], F32, name="bank")
-        nc.tensor.transpose(vec_turn[:, 0, :], vec_wide[:], ident[:])
-        nc.scalar.copy(out=vec_col[:], in_=vec_turn[:, 0, 0:24])
-        for i in range(EARLY_TANH):
-            r_tanh(r_units[i], first[i])
-        for i in range(TILES, LEAD):
-            first.append(r_product(r_units[i]))
-        for j in range(TILES):
-            interleave(0, j, 1, False)
-        widen_first(2)
-        interleave(0, 0, 2, False)
-        widen_first(3)
-        interleave(0, 1, 2, False)
-        interleave(0, 0, 3, False)
-        interleave(0, 1, 3, False)
-        quantize_u(0, 0)
-        for i in range(EARLY_TANH, LEAD):
-            r_tanh(r_units[i], first[i])
+        quantize_u(1, 0, 0, TILES)
+        nc.tensor.transpose(spread[:, 1, :], vec_wide[:], ident[:])
+        nc.scalar.copy(out=vec_col[:], in_=spread[:, 1, 0:24])
+        done = []
 
-        pieces = [("i", 0, 2, 2), ("q", 0, 1, 0), ("i", 0, 2, 3), ("i", 0, 3, 2), ("q", 0, 2, 0)]
-        pieces = pieces + [("i", 0, 3, 3), ("i", 1, 0, 0), ("q", 0, 3, 0)]
-        pieces = pieces + [("i", 1, j, c) for c in range(PASSES - 1) for j in range(TILES)][1:]
-        for j in range(TILES):
-            pieces.append(("i", 1, j, PASSES - 1))
-            if j > 0:
-                pieces.append(("q", 1, j - 1, 0))
-        pieces.append(("q", 1, TILES - 1, 0))
+        def tanh_until(count):
+            for i in range(len(done), count):
+                r_tanh(r_units[i], first[i])
+                done.append(i)
+
+        tanh_until(1)
+        first = first + r_four(r_units[4:8])
+        widen_first(1)
+        tanh_until(TANH_AT[0])
+        finish(0, 1)
+        widen_first(2)
+        tanh_until(TANH_AT[1])
+        quantize_u(0, 1, 0, TILES)
+        finish(0, 2)
+        tanh_until(4)
+        if LEAD == 12:
+            first = first + r_four(r_units[8:12])
+        widen_first(3)
+        quantize_u(0, 2, 0, TILES)
+        interleave(0, 3, 0, False)
+        interleave(0, 3, 1, False)
+        quantize_u(0, 3, 0, 1)
+        interleave(0, 3, 2, False)
+        interleave(0, 3, 3, False)
+        quantize_u(0, 3, 1, 2)
+        tanh_until(8)
+        widen_late(TANH_AT[2])
+        tanh_until(10)
+        widen_late(TANH_AT[3])
+        tanh_until(LEAD)
+        quantize_u(0, 3, 2, TILES)
+
+        pieces = []
+        for c in range(1, PASSES):
+            for j in range(TILES):
+                pieces.append(("i", c, j))
+                if j == 0 and c > 1:
+                    pieces.append(("q", c - 1, 0))
+        pieces.append(("q", PASSES - 1, 0))
 
         def prepare(count):
             for piece in pieces[:count]:
-                kind, g, j, c = piece
+                kind, c, j = piece
+                if (c, PACK - 1) in late_rows:
+                    return
                 if kind == "i":
-                    interleave(g, j, c, g == 1 and j >= SCALAR_TILE and c < PASSES - 1)
+                    interleave(1, c, j, j >= TILES - S_BLOCKS)
                 else:
-                    quantize_u(g, j)
+                    quantize_u(1, c, 0, TILES)
                 pieces.remove(piece)
 
         groups = [(g, h) for g in range(2) for h in range(2)]
-        prepare(2)
         for s in range(steps - 2):
             unit = u_units[s]
             u_product(unit)
             subtract(unit)
-            if s >= 4 and s % 2 == 0:
+            if 4 <= s <= BOTH_FROM and s % 2 == 0:
                 round_y(u_units[s - 4], False, False)
             elif s >= 9 and s % 4 == 1:
                 quantize_y(*groups[s // 4 - 2])
@@ -354,16 +393,20 @@ def tile_distillation_curiosity_terms_b7_kernel(
                 round_y(u_units[s - 3], False, False)
             if s == 13:
                 store_plane(0)
+            widen_late(S_RATE * WIDE_FIRST)
             if s + LEAD < steps:
                 r_tanh(r_units[s + LEAD], r_product(r_units[s + LEAD]))
-            widen_late(WIDEN_PER_STEP)
-            prepare(PIECES_PER_STEP)
+            widen_late(S_RATE * (1 - WIDE_FIRST))
+            prepare(V_RATE)
             if s >= 3 and s % 2 == 1:
                 turn_y(u_units[s - 3])
                 turn_y(u_units[s - 2])
                 if s >= 7 and s % 4 == 3:
-                    turn_pairs(*groups[s // 4 - 1])
+                    for i in range(2):
+                        turn_pairs(*groups[s // 4 - 1], i)
                 copy_y(u_units[s - 3])
+                if s >= BOTH_FROM:
+                    round_y(u_units[s - 3], True, True)
                 copy_y(u_units[s - 2])
                 if s >= SCALAR_ROUND_FROM:
                     round_y(u_units[s - 2], True, True)
@@ -377,32 +420,53 @@ def tile_distillation_curiosity_terms_b7_kernel(
         last = u_units[12:]
         u_product(last[2])
         subtract(last[2])
-        round_y(u_units[10], False, False)
         weigh(last[2])
         turn_y(last[0])
         turn_y(last[1])
         copy_y(last[0])
         copy_y(last[1])
         store_y(1, 1, 0, 2)
-        u_product(last[3])
-        subtract(last[3])
+        if TAIL == 1:
+            for i in range(2):
+                turn_pairs(1, 0, i)
+                copy_pairs(1, 0, i, True)
         round_y(last[0], False, False)
-        weigh(last[3])
-        turn_pairs(1, 0)
-        turn_y(last[2])
+        u_product(last[3], 0, 2)
+        u_product(last[3], 2, 4)
+        subtract(last[3], 0, 2)
         round_y(last[1], False, False)
+        weigh(last[3], 0, 2)
+        subtract(last[3], 2, 4)
+        turn_y(last[2])
+        round_y(last[2], True, True)
         copy_y(last[2])
         store_y(1, 1, 2, 3)
-        round_y(last[2], False, False)
-        turn_y(last[3])
-        copy_pairs(1, 0, 0, True)
-        round_y(last[3], False, True)
-        copy_pairs(1, 0, 1, True)
-        copy_y(last[3])
+        turn_y(last[3], 0, 2)
+        if TAIL == 1:
+            quantize_y(1, 0)
+        weigh(last[3], 2, 4)
+        round_y(last[3], False, True, 0, 2)
+        if TAIL == 0:
+            turn_pairs(1, 0, 0)
+        turn_y(last[3], 2, 4)
+        if TAIL == 0:
+            turn_pairs(1, 0, 1)
+        round_y(last[3], False, True, 2, 4)
+        if TAIL == 0:
+            copy_pairs(1, 0, 0, True)
+        copy_y(last[3], 0, 2)
+        copy_y(last[3], 2, 4)
         store_y(1, 1, 3, 4)
-        turn_pairs(1, 1)
-        quantize_y(1, 0)
-        copy_pairs(1, 1, 0, False)
-        copy_pairs(1, 1, 1, True)
-        quantize_y(1, 1)
+        turn_pairs(1, 1, 0)
+        turn_pairs(1, 1, 1)
+        if TAIL == 0:
+            copy_pairs(1, 0, 1, False)
+            copy_pairs(1, 1, 0, True)
+            quantize_y(1, 0)
+            copy_pairs(1, 1, 1, True)
+        else:
+            copy_pairs(1, 1, 0, False)
+            copy_pairs(1, 1, 1, True)
+        quantize_y(1, 1, 0, 2)
+        quantize_y(1, 1, 2, 4)
         store_plane(1)

@@ -21,26 +21,18 @@ P = 128
 PACK = 4
 PASSES = K // (P * PACK)
 HALF = 512
-TILES = HALF // P
-LEAD = 12
+BLOCKS = HALF // P
+QUADRANTS = 4
 RUN = 4
-ORDER = "x1 x2 r0 x3 v r1 u1 r2 u2 y0 u3 y1"
-U_FIRST = 1
-V_ROWS = (3, 3, 2, 2)
-V_RATE = 2
-S_RATE = 2
-S_BLOCKS = 0
-SCALAR_ROUND_FROM = 2
-TANH_AT = (4, 4, 4, 4)
-BOTH_FROM = 2
-TAIL = 0
-WIDE_FIRST = 1
+LEAD = 12
+JOBS_AFTER_UNIT = 2
 
 
 def tile_distillation_curiosity_terms_b7_kernel(
     tc, x_words, x_scales, U_bytes, U_scale, R_words, R_scales, u_bias, r_bias, feat_weight, out_0, out_1, out_2
 ):
     nc = tc.nc
+    on_vector, on_scalar = nc.vector.tensor_copy, nc.scalar.copy
     with ExitStack() as ctx:
         keep = ctx.enter_context(tc.tile_pool(name="keep", bufs=1))
         work = ctx.enter_context(tc.tile_pool(name="work", bufs=2))
@@ -49,222 +41,205 @@ def tile_distillation_curiosity_terms_b7_kernel(
 
         x_plane = keep.tile([P, PASSES, T], U8, name="x_plane", align_bytes=64)
         r_plane = keep.tile([P, PASSES, N], U8, name="r_plane", align_bytes=64)
-        nc.vector.memset(x_plane[:].rearrange("p g n -> p (g n)").bitcast(I32), 0)
-        nc.vector.memset(r_plane[:].rearrange("p g n -> p (g n)").bitcast(I32), 0)
+        nc.vector.memset(x_plane[:].rearrange("p c n -> p (c n)").bitcast(I32), 0)
+        nc.vector.memset(r_plane[:].rearrange("p c n -> p (c n)").bitcast(I32), 0)
 
-        ident = keep.tile([P, P], F32, name="ident")
         scale_flat = keep.tile([P, 1], F32, name="scale_flat")
+        nc.gpsimd.dma_start(out=scale_flat[:], in_=U_scale.rearrange("i (j o) -> (i j) o", o=1))
+        ident = keep.tile([P, P], F32, name="ident")
+        make_identity(nc, ident[:])
         vec_rows = keep.tile([P, P], BF16, name="vec_rows")
-
-        warm = keep.tile([P, 1], F32, name="warm")
-        nc.vector.memset(warm[:], 0.0)
-        warm_out = keep.tile([P, 1], F32, name="warm_out")
-        nc.scalar.activation(out=warm_out[:], in_=warm[:], func=ACT.Tanh)
+        nc.gpsimd.memset(vec_rows[:], 0.0)
+        rows_per_vec = N // P
 
         u_raw, x_code, r_code = {}, {}, {}
-        x_rows = x_words.rearrange("g p n t -> p g (n t)")
-        r_rows = R_words.rearrange("g p b -> p g b")
+        x_rows = x_words.rearrange("c p n t -> p c (n t)")
+        r_rows = R_words.rearrange("c p b -> p c b")
 
         def load_u(c):
             u_raw[c] = keep.tile([P, PACK, N], U8, name="u_raw_%d" % c)
-            rows = U_bytes[c * 512 : (c + 1) * 512, :]
+            rows = U_bytes[c * P * PACK : (c + 1) * P * PACK, :]
             nc.sync.dma_start(out=u_raw[c][:], in_=rows.rearrange("(p t) n -> p t n", t=PACK))
 
         def load_x(h, c0, c1):
             words = keep.tile([P, c1 - c0, HALF], U32, name="x_code_%d_%d" % (h, c0), align_bytes=64)
-            nc.sync.dma_start(
-                out=words[:].bitcast(I32), in_=x_rows[:, c0:c1, h * HALF * 4 : (h + 1) * HALF * 4].bitcast(I32)
-            )
+            src = x_rows[:, c0:c1, h * HALF * PACK : (h + 1) * HALF * PACK]
+            nc.sync.dma_start(out=words[:].bitcast(I32), in_=src.bitcast(I32))
             for c in range(c0, c1):
                 x_code[h, c] = words[:, c - c0, :]
 
         def load_r(g, c0, c1):
             words = keep.tile([P, c1 - c0, 2 * HALF], U8, name="r_code_%d_%d" % (g, c0), align_bytes=64)
-            nc.sync.dma_start(
-                out=words[:].bitcast(I32), in_=r_rows[:, c0:c1, g * HALF * 2 : (g + 1) * HALF * 2].bitcast(I32)
-            )
+            src = r_rows[:, c0:c1, g * HALF * 2 : (g + 1) * HALF * 2]
+            nc.sync.dma_start(out=words[:].bitcast(I32), in_=src.bitcast(I32))
             for c in range(c0, c1):
                 r_code[g, c] = words[:, c - c0, :]
 
-        def load_plane(queue, plane, scales, q):
-            queue.dma_start(
-                out=plane[32 * q : 32 * q + 4, :, :].bitcast(I32),
-                in_=scales[:, 4 * q : 4 * q + 4, :].rearrange("g r n -> r g n").bitcast(I32),
-            )
+        def load_plane(plane, scales, q0, q1):
+            for q in range(q0, q1):
+                src = scales[:, 4 * q : 4 * q + 4, :].rearrange("c r n -> r c n")
+                nc.sync.dma_start(out=plane[32 * q : 32 * q + 4, :, :].bitcast(I32), in_=src.bitcast(I32))
 
-        nc.gpsimd.dma_start(out=scale_flat[:], in_=U_scale.rearrange("i (j o) -> (i j) o", o=1))
-        make_identity(nc, ident[:])
-        nc.gpsimd.memset(vec_rows[:], 0.0)
         load_x(0, 0, 1)
         load_r(0, 0, 2)
-        load_plane(nc.sync, x_plane, x_scales, 0)
-        if U_FIRST:
-            load_u(0)
-        for q in range(1, 4):
-            load_plane(nc.sync, x_plane, x_scales, q)
-        for q in range(4):
-            load_plane(nc.sync, r_plane, R_scales, q)
-        for item in ORDER.split():
-            if item == "v":
-                for i, vec in enumerate((r_bias, u_bias, feat_weight)):
-                    nc.sync.dma_start(out=vec_rows[8 * i : 8 * i + 8, :], in_=vec.rearrange("o (j p) -> (o j) p", p=P))
-            elif item[0] == "u":
-                load_u(int(item[1]))
-            elif item[0] == "x":
-                load_x(0, int(item[1]), int(item[1]) + 1)
-            elif item[0] == "y":
-                load_x(1, 2 * int(item[1]), 2 * int(item[1]) + 2)
-            elif item == "r0":
-                load_r(0, 2, 4)
-            elif item == "r1":
-                load_r(1, 0, 2)
-            else:
-                load_r(1, 2, 4)
+        load_plane(x_plane, x_scales, 0, 1)
+        load_u(0)
+        load_plane(x_plane, x_scales, 1, QUADRANTS)
+        load_plane(r_plane, R_scales, 0, QUADRANTS)
+        load_x(0, 1, 2)
+        load_x(0, 2, 3)
+        load_r(0, 2, 4)
+        for i, vec in enumerate((r_bias, u_bias, feat_weight)):
+            rows = vec_rows[rows_per_vec * i : rows_per_vec * (i + 1), :]
+            nc.sync.dma_start(out=rows, in_=vec.rearrange("o (j p) -> (o j) p", p=P))
+        load_x(0, 3, 4)
+        load_r(1, 0, 2)
+        load_u(1)
+        load_r(1, 2, 4)
+        load_u(2)
+        load_x(1, 0, 2)
+        load_u(3)
+        load_x(1, 2, 4)
 
         u_wide, u_grp, u_code, u_plane = {}, {}, {}, {}
-        scale_col = keep.tile([P, PASSES, 8], F32, name="scale_col")
-        vec_col = keep.tile([P, 24], F32, name="vec_col")
+        scale_col = keep.tile([P, PASSES, N // P], F32, name="scale_col")
+        vec_col = keep.tile([P, 3 * rows_per_vec], F32, name="vec_col")
 
-        def pick_scales():
-            nc.tensor.transpose(spread[:, 0, :], scale_flat[:].to_broadcast([P, P]), ident[:])
-            by_quadrant = spread[:, 0, :].rearrange("p (c q j) -> p q c j", q=4, j=8)
-            for q in range(4):
-                rows = slice(32 * q, 32 * q + 32)
-                nc.vector.tensor_copy(out=scale_col[rows, :, :], in_=by_quadrant[rows, q, :, :])
-
-        def widen(g, c, t, on_scalar):
-            if (g, c) not in u_wide:
+        def widen(g, c, t0, t1, copy):
+            if t0 == 0:
                 u_wide[g, c] = keep.tile([P, PACK, HALF], BF16, name="u_wide_%d_%d" % (g, c))
-            src = u_raw[c][:, t, g * HALF : (g + 1) * HALF].bitcast(FP8)
-            if on_scalar:
-                nc.scalar.copy(out=u_wide[g, c][:, t, :], in_=src)
-            else:
-                nc.vector.tensor_copy(out=u_wide[g, c][:, t, :], in_=src)
+            for t in range(t0, t1):
+                copy(out=u_wide[g, c][:, t, :], in_=u_raw[c][:, t, g * HALF : (g + 1) * HALF].bitcast(FP8))
 
-        def interleave(g, c, j, on_scalar):
-            if (g, c) not in u_grp:
-                u_grp[g, c] = work.tile([P, TILES, P, PACK], BF16, name="u_grp", bufs=3, align_bytes=64)
-            src = u_wide[g, c][:, :, j * P : (j + 1) * P].rearrange("p t (a i) -> p a t i", i=RUN)
-            dst = u_grp[g, c][:, j, :, :].rearrange("p (a i) t -> p a t i", i=RUN)
-            col = scale_col[:, c, g * TILES + j : g * TILES + j + 1]
-            if on_scalar:
-                nc.scalar.activation(out=dst, in_=src, func=ACT.Copy, scale=col)
-            else:
-                nc.vector.tensor_scalar(out=dst, in0=src, scalar1=col, scalar2=None, op0=ALU.mult)
+        def interleave(g, c, j):
+            if j == 0:
+                u_grp[g, c] = work.tile([P, BLOCKS, P, PACK], BF16, name="u_grp", bufs=3, align_bytes=64)
+            nc.vector.tensor_scalar(
+                out=u_grp[g, c][:, j, :, :].rearrange("p (a i) t -> p a t i", i=RUN),
+                in0=u_wide[g, c][:, :, j * P : (j + 1) * P].rearrange("p t (a i) -> p a t i", i=RUN),
+                scalar1=scale_col[:, c, g * BLOCKS + j : g * BLOCKS + j + 1],
+                scalar2=None,
+                op0=ALU.mult,
+            )
 
-        def quantize_u(g, c, j0, j1):
-            if (g, c) not in u_code:
-                u_code[g, c] = keep.tile([P, TILES, P], U32, name="u_code_%d_%d" % (g, c), align_bytes=64)
-                u_plane[g, c] = keep.tile([P, TILES, P], U8, name="u_plane_%d_%d" % (g, c), align_bytes=64)
+        def quantize_u(g, c, j0=0, j1=BLOCKS):
+            if j0 == 0:
+                u_code[g, c] = keep.tile([P, BLOCKS, P], U32, name="u_code_%d_%d" % (g, c), align_bytes=64)
+                u_plane[g, c] = keep.tile([P, BLOCKS, P], U8, name="u_plane_%d_%d" % (g, c), align_bytes=64)
             nc.vector.quantize_mx(
                 out=u_code[g, c][:, j0:j1, :].rearrange("p j n -> p (j n)").bitcast(FP8X4),
                 scales=u_plane[g, c][:, j0:j1, :].rearrange("p j n -> p (j n)"),
                 in_=u_grp[g, c][:, j0:j1, :, :].rearrange("p j n t -> p (j n t)"),
             )
 
-        target, diff, y_feat, y_tok, y_pairs, y_grp, turned, pred = {}, {}, {}, {}, {}, {}, {}, {}
-        y_plane = keep.tile([P, 2, T], U8, name="y_plane", align_bytes=64)
+        r_bank, target, pred, diff, y_feat, y_turned = {}, {}, {}, {}, {}, {}
+        y_tok, y_pairs, pairs_turned, y_grp = {}, {}, {}, {}
+        y_plane = keep.tile([P, N // HALF, T], U8, name="y_plane", align_bytes=64)
 
-        def mx_pass(acc, h, c, weights, plane, b0=0, b1=TILES):
+        def mx_pass(acc, h, c, weights, weight_scales, b0, b1):
             nc.tensor.matmul_mx(
                 out=acc[:],
                 lhsT=weights,
-                lhsT_scale=plane,
+                lhsT_scale=weight_scales,
                 rhs=x_code[h, c][:, b0 * P : b1 * P].bitcast(FP8X4),
                 rhs_scale=x_plane[:, c, h * HALF + b0 * P : h * HALF + b1 * P],
                 start=(c == 0),
                 stop=(c == PASSES - 1),
             )
 
-        def column(which, g, j):
-            i = 8 * which + g * TILES + j
-            return vec_col[:, i : i + 1]
+        def column(i, unit):
+            n = rows_per_vec * i + unit[0] * BLOCKS + unit[1]
+            return vec_col[:, n : n + 1]
 
-        def r_pass(unit, acc, c):
-            g, j, h = unit
-            n0 = g * HALF + j * P
-            mx_pass(acc, h, c, r_code[g, c][:, 2 * j * P : 2 * (j + 1) * P].bitcast(FP4X4), r_plane[:, c, n0 : n0 + P])
+        def r_products(units, c0=0, c1=PASSES):
+            if c0 == 0:
+                for unit in units:
+                    r_bank[unit] = psum.tile([P, HALF], F32, name="bank")
+            for c in range(c0, c1):
+                for g, j, h in units:
+                    weights = r_code[g, c][:, 2 * j * P : 2 * (j + 1) * P].bitcast(FP4X4)
+                    n0 = g * HALF + j * P
+                    mx_pass(r_bank[g, j, h], h, c, weights, r_plane[:, c, n0 : n0 + P], 0, BLOCKS)
 
-        def r_product(unit):
-            acc = psum.tile([P, HALF], F32, name="bank")
-            for c in range(PASSES):
-                r_pass(unit, acc, c)
-            return acc
+        def tanh(units):
+            for unit in units:
+                target[unit] = work.tile([P, HALF], F32, name="target", bufs=LEAD)
+                nc.scalar.activation(out=target[unit][:], in_=r_bank[unit][:], func=ACT.Tanh, bias=column(0, unit))
 
-        def r_tanh(unit, acc):
-            g, j, h = unit
-            target[unit] = work.tile([P, HALF], F32, name="target", bufs=12)
-            nc.scalar.activation(out=target[unit][:], in_=acc[:], func=ACT.Tanh, bias=column(0, g, j))
-
-        def u_product(unit, b0=0, b1=TILES):
+        def u_product(unit, b0=0, b1=BLOCKS):
             g, j, h = unit
             pred[unit, b0] = psum.tile([P, (b1 - b0) * P], F32, name="bank")
             for c in range(PASSES):
                 mx_pass(pred[unit, b0], h, c, u_code[g, c][:, j, :].bitcast(FP8X4), u_plane[g, c][:, j, :], b0, b1)
 
-        def subtract(unit, b0=0, b1=TILES):
-            g, j, h = unit
-            diff[unit, b0] = work.tile([P, (b1 - b0) * P], F32, name="diff", bufs=2)
+        def subtract(unit, b0=0, b1=BLOCKS):
+            diff[unit, b0] = work.tile([P, (b1 - b0) * P], F32, name="diff")
             nc.vector.scalar_tensor_tensor(
-                out=diff[unit, b0][:], in0=pred[unit, b0][:], scalar=column(1, g, j),
-                in1=target[unit][:, b0 * P : b1 * P], op0=ALU.add, op1=ALU.subtract,
+                out=diff[unit, b0][:],
+                in0=pred[unit, b0][:],
+                scalar=column(1, unit),
+                in1=target[unit][:, b0 * P : b1 * P],
+                op0=ALU.add,
+                op1=ALU.subtract,
             )
 
-        def weigh(unit, b0=0, b1=TILES):
-            g, j, h = unit
+        def weigh(unit, b0=0, b1=BLOCKS):
             y_feat[unit, b0] = work.tile([P, (b1 - b0) * P], F32, name="y_feat", bufs=5)
             nc.vector.scalar_tensor_tensor(
-                out=y_feat[unit, b0][:], in0=diff[unit, b0][:], scalar=column(2, g, j), in1=diff[unit, b0][:],
-                op0=ALU.mult, op1=ALU.mult,
+                out=y_feat[unit, b0][:],
+                in0=diff[unit, b0][:],
+                scalar=column(2, unit),
+                in1=diff[unit, b0][:],
+                op0=ALU.mult,
+                op1=ALU.mult,
             )
 
-        def turn_y(unit, b0=0, b1=TILES):
-            turned[unit, b0] = psum.tile([P, b1 - b0, P], F32, name="bank")
+        def turn_y(unit, b0=0, b1=BLOCKS):
+            y_turned[unit, b0] = psum.tile([P, b1 - b0, P], F32, name="bank")
             for b in range(b1 - b0):
-                nc.tensor.transpose(turned[unit, b0][:, b, :], y_feat[unit, b0][:, b * P : (b + 1) * P], ident[:])
+                nc.tensor.transpose(y_turned[unit, b0][:, b, :], y_feat[unit, b0][:, b * P : (b + 1) * P], ident[:])
 
-        def copy_y(unit, b0=0, b1=TILES):
+        def copy_y(unit, b0=0, b1=BLOCKS):
             g, j, h = unit
-            if (g, h) not in y_tok:
-                y_tok[g, h] = work.tile([P, TILES, HALF], F32, name="y_tok", bufs=3)
-            nc.scalar.copy(out=y_tok[g, h][:, b0:b1, j * P : (j + 1) * P], in_=turned[unit, b0][:])
+            if j == 0:
+                y_tok[g, h] = work.tile([P, BLOCKS, HALF], F32, name="y_tok", bufs=3)
+            nc.scalar.copy(out=y_tok[g, h][:, b0:b1, j * P : (j + 1) * P], in_=y_turned[unit, b0][:])
 
         def store_y(g, h, j0, j1):
             rows = out_0[h * HALF : (h + 1) * HALF, g * HALF + j0 * P : g * HALF + j1 * P]
             nc.sync.dma_start(out=rows.rearrange("(b p) n -> p b n", p=P), in_=y_tok[g, h][:, :, j0 * P : j1 * P])
 
-        def round_y(unit, on_scalar, from_bank, b0=0, b1=TILES):
+        def pair_views(unit, src, b0, b1):
             g, j, h = unit
-            if (g, h) not in y_pairs:
-                y_pairs[g, h] = work.tile([P, TILES, 2, P, 2], BF16, name="y_pairs", bufs=2)
-            dst = y_pairs[g, h][:, b0:b1, :, 32 * j : 32 * j + 32, :]
-            src = turned[unit, b0][:] if from_bank else y_tok[g, h][:, b0:b1, j * P : (j + 1) * P]
-            src = src.rearrange("p b (q u e) -> p b u q e", u=2, e=2)
-            if on_scalar:
-                nc.scalar.copy(out=dst, in_=src)
-            else:
-                nc.vector.tensor_copy(out=dst, in_=src)
+            if j == 0:
+                y_pairs[g, h] = work.tile([P, BLOCKS, 2, P, 2], BF16, name="y_pairs")
+            words = P // PACK
+            dst = y_pairs[g, h][:, b0:b1, :, words * j : words * (j + 1), :]
+            return dst, src.rearrange("p b (q u e) -> p b u q e", u=2, e=2)
+
+        def round_on_scalar(unit):
+            dst, src = pair_views(unit, y_turned[unit, 0][:], 0, BLOCKS)
+            nc.scalar.copy(out=dst, in_=src)
+
+        def round_on_vector(unit, src, b0=0, b1=BLOCKS):
+            dst, src = pair_views(unit, src, b0, b1)
+            nc.vector.tensor_copy(out=dst, in_=src)
 
         def turn_pairs(g, h, i):
             words = y_pairs[g, h][:, 2 * i : 2 * i + 2].rearrange("p b u q e -> p (b u q e)").bitcast(F32)
-            bank = psum.tile([P, 2, 2, P], F32, name="bank")
-            turned[g, h, i, "pairs"] = bank
+            pairs_turned[g, h, i] = psum.tile([P, 2, 2, P], F32, name="bank")
             for b in range(2):
                 for u in range(2):
-                    w0 = (b * 2 + u) * P
-                    nc.tensor.transpose(bank[:, b, u, :], words[:, w0 : w0 + P], ident[:])
+                    w0 = (2 * b + u) * P
+                    nc.tensor.transpose(pairs_turned[g, h, i][:, b, u, :], words[:, w0 : w0 + P], ident[:])
 
-        def copy_pairs(g, h, i, on_scalar):
-            if (g, h) not in y_grp:
-                y_grp[g, h] = work.tile([P, HALF * PACK], BF16, name="y_grp", bufs=2, align_bytes=64)
+        def copy_pairs(g, h, i, copy):
+            if i == 0:
+                y_grp[g, h] = work.tile([P, HALF * PACK], BF16, name="y_grp", align_bytes=64)
             words = y_grp[g, h][:].bitcast(F32).rearrange("p (i b r u) -> p i b r u", i=2, b=2, u=2)
-            src = turned[g, h, i, "pairs"][:].rearrange("p b u r -> p b r u")
-            if on_scalar:
-                nc.scalar.copy(out=words[:, i, :, :, :], in_=src)
-            else:
-                nc.vector.tensor_copy(out=words[:, i, :, :, :], in_=src)
+            copy(out=words[:, i, :, :, :], in_=pairs_turned[g, h, i][:].rearrange("p b u r -> p b r u"))
 
-        def quantize_y(g, h, b0=0, b1=TILES):
+        def quantize_y(g, h, b0=0, b1=BLOCKS):
             codes = work.tile([P, (b1 - b0) * P], U32, name="y_code", bufs=3, align_bytes=64)
             m0, m1 = h * HALF + b0 * P, h * HALF + b1 * P
             nc.vector.quantize_mx(
@@ -272,201 +247,150 @@ def tile_distillation_curiosity_terms_b7_kernel(
                 scales=y_plane[:, g, m0:m1],
                 in_=y_grp[g, h][:, b0 * P * PACK : b1 * P * PACK],
             )
-            dst = out_1[g].rearrange("p m t -> p (m t)")[:, m0 * 4 : m1 * 4]
+            dst = out_1[g].rearrange("p m t -> p (m t)")[:, m0 * PACK : m1 * PACK]
             nc.sync.dma_start(out=dst.bitcast(I32), in_=codes[:].bitcast(I32))
 
         def store_plane(g):
-            for q in range(4):
-                nc.sync.dma_start(
-                    out=out_2[g, 4 * q : 4 * q + 4, :].bitcast(I32), in_=y_plane[32 * q : 32 * q + 4, g, :].bitcast(I32)
-                )
+            for q in range(QUADRANTS):
+                src = y_plane[32 * q : 32 * q + 4, g, :]
+                nc.sync.dma_start(out=out_2[g, 4 * q : 4 * q + 4, :].bitcast(I32), in_=src.bitcast(I32))
 
-        r_units = [(g, j, h) for h in range(2) for g in range(2) for j in range(TILES)]
-        u_units = [(g, j, h) for g in range(2) for h in range(2) for j in range(TILES)]
-        steps = len(u_units)
-        late_rows = [(c, t) for c in range(PASSES) for t in range(PACK)]
-
-        def widen_late(count):
-            for c, t in late_rows[:count]:
-                widen(1, c, t, True)
-                late_rows.remove((c, t))
-
-        def r_four(units):
-            banks = []
-            for i in range(TILES):
-                acc = psum.tile([P, HALF], F32, name="bank")
-                banks.append(acc)
-            for c in range(PASSES):
-                for i in range(TILES):
-                    r_pass(units[i], banks[i], c)
-            return banks
-
-        def widen_first(c):
-            for t in range(PACK):
-                widen(0, c, t, t >= V_ROWS[c])
-
-        def finish(g, c):
-            for j in range(TILES):
-                interleave(g, c, j, False)
-
-        spread = psum.tile([P, TILES, P], F32, name="bank")
-        pick_scales()
-        first = r_four(r_units[0:4])
-        widen_first(0)
-        widen_late(PACK)
-        finish(0, 0)
-        interleave(1, 0, 0, False)
-        quantize_u(0, 0, 0, TILES)
-        for j in range(1, TILES):
-            interleave(1, 0, j, False)
-        vec_wide = keep.tile([P, P], F32, name="vec_wide")
-        nc.vector.tensor_copy(out=vec_wide[:], in_=vec_rows[:])
-        quantize_u(1, 0, 0, TILES)
-        nc.tensor.transpose(spread[:, 1, :], vec_wide[:], ident[:])
-        nc.scalar.copy(out=vec_col[:], in_=spread[:, 1, 0:24])
-        done = []
-
-        def tanh_until(count):
-            for i in range(len(done), count):
-                r_tanh(r_units[i], first[i])
-                done.append(i)
-
-        tanh_until(1)
-        first = first + r_four(r_units[4:8])
-        widen_first(1)
-        tanh_until(TANH_AT[0])
-        finish(0, 1)
-        widen_first(2)
-        tanh_until(TANH_AT[1])
-        quantize_u(0, 1, 0, TILES)
-        finish(0, 2)
-        tanh_until(4)
-        if LEAD == 12:
-            first = first + r_four(r_units[8:12])
-        widen_first(3)
-        quantize_u(0, 2, 0, TILES)
-        interleave(0, 3, 0, False)
-        interleave(0, 3, 1, False)
-        quantize_u(0, 3, 0, 1)
-        interleave(0, 3, 2, False)
-        interleave(0, 3, 3, False)
-        quantize_u(0, 3, 1, 2)
-        tanh_until(8)
-        widen_late(TANH_AT[2])
-        tanh_until(10)
-        widen_late(TANH_AT[3])
-        tanh_until(LEAD)
-        quantize_u(0, 3, 2, TILES)
-
-        pieces = []
-        for c in range(1, PASSES):
-            for j in range(TILES):
-                pieces.append(("i", c, j))
-                if j == 0 and c > 1:
-                    pieces.append(("q", c - 1, 0))
-        pieces.append(("q", PASSES - 1, 0))
-
-        def prepare(count):
-            for piece in pieces[:count]:
-                kind, c, j = piece
-                if (c, PACK - 1) in late_rows:
-                    return
-                if kind == "i":
-                    interleave(1, c, j, j >= TILES - S_BLOCKS)
-                else:
-                    quantize_u(1, c, 0, TILES)
-                pieces.remove(piece)
-
+        r_units = [(g, j, h) for h in range(2) for g in range(2) for j in range(BLOCKS)]
+        u_units = [(g, j, h) for g in range(2) for h in range(2) for j in range(BLOCKS)]
         groups = [(g, h) for g in range(2) for h in range(2)]
-        for s in range(steps - 2):
-            unit = u_units[s]
+
+        spread = psum.tile([P, 2, P], F32, name="bank")
+        nc.tensor.transpose(spread[:, 0, :], scale_flat[:].to_broadcast([P, P]), ident[:])
+        by_quadrant = spread[:, 0, :].rearrange("p (c q j) -> p q c j", q=QUADRANTS, j=N // P)
+        for q in range(QUADRANTS):
+            rows = slice(32 * q, 32 * q + 32)
+            nc.vector.tensor_copy(out=scale_col[rows, :, :], in_=by_quadrant[rows, q, :, :])
+
+        last_pass = PASSES - 1
+        r_products(r_units[0:4], 0, last_pass)
+        vec_wide = keep.tile([P, P], F32, name="vec_wide")
+        nc.gpsimd.tensor_copy(out=vec_wide[:], in_=vec_rows[:])
+        nc.tensor.transpose(spread[:, 1, :], vec_wide[:], ident[:])
+        r_products(r_units[0:4], last_pass, PASSES)
+
+        widen(0, 0, 0, PACK, on_vector)
+        widen(1, 0, 0, PACK, on_scalar)
+        for j in range(BLOCKS):
+            interleave(0, 0, j)
+        interleave(1, 0, 0)
+        quantize_u(0, 0)
+        for j in range(1, BLOCKS):
+            interleave(1, 0, j)
+        quantize_u(1, 0)
+        widen(0, 1, 0, PACK, on_vector)
+
+        nc.scalar.copy(out=vec_col[:], in_=spread[:, 1, 0 : 3 * rows_per_vec])
+        tanh(r_units[0:4])
+        r_products(r_units[4:8])
+        r_products(r_units[8:LEAD])
+
+        for c in range(1, last_pass):
+            for j in range(BLOCKS):
+                interleave(0, c, j)
+            widen(0, c + 1, 0, PACK - 1, on_vector)
+            widen(0, c + 1, PACK - 1, PACK, on_scalar)
+            quantize_u(0, c)
+        interleave(0, last_pass, 0)
+        interleave(0, last_pass, 1)
+        quantize_u(0, last_pass, 0, 1)
+        interleave(0, last_pass, 2)
+        interleave(0, last_pass, 3)
+        quantize_u(0, last_pass, 1, 2)
+        quantize_u(0, last_pass, 2, BLOCKS)
+
+        tanh(r_units[4:8])
+        widen(1, 1, 0, PACK, on_scalar)
+        tanh(r_units[8:10])
+        widen(1, 2, 0, PACK, on_scalar)
+        tanh(r_units[10:LEAD])
+        widen(1, 3, 0, PACK, on_scalar)
+
+        jobs = []
+        for c in range(1, PASSES):
+            jobs.append((interleave, c, 0))
+            if c > 1:
+                jobs.append((quantize_u, c - 1, 0))
+            jobs.extend([(interleave, c, j) for j in range(1, BLOCKS)])
+        jobs.append((quantize_u, last_pass, 0))
+
+        def run_jobs(count):
+            for job in jobs[:count]:
+                job[0](1, job[1], job[2])
+                jobs.remove(job)
+
+        for s, unit in enumerate(u_units[:-2]):
             u_product(unit)
             subtract(unit)
-            if 4 <= s <= BOTH_FROM and s % 2 == 0:
-                round_y(u_units[s - 4], False, False)
-            elif s >= 9 and s % 4 == 1:
-                quantize_y(*groups[s // 4 - 2])
+            if s > 2 * BLOCKS and s % BLOCKS == 1:
+                quantize_y(*groups[s // BLOCKS - 2])
+                if groups[s // BLOCKS - 2] == (0, 1):
+                    store_plane(0)
             else:
-                prepare(1)
+                run_jobs(1)
             weigh(unit)
-            if 4 <= s <= SCALAR_ROUND_FROM and s % 2 == 0:
-                round_y(u_units[s - 3], False, False)
-            if s == 13:
-                store_plane(0)
-            widen_late(S_RATE * WIDE_FIRST)
-            if s + LEAD < steps:
-                r_tanh(r_units[s + LEAD], r_product(r_units[s + LEAD]))
-            widen_late(S_RATE * (1 - WIDE_FIRST))
-            prepare(V_RATE)
+            if s + LEAD < len(r_units):
+                r_products(r_units[s + LEAD : s + LEAD + 1])
+                tanh(r_units[s + LEAD : s + LEAD + 1])
+            run_jobs(JOBS_AFTER_UNIT)
             if s >= 3 and s % 2 == 1:
-                turn_y(u_units[s - 3])
-                turn_y(u_units[s - 2])
-                if s >= 7 and s % 4 == 3:
+                pair_run = s > BLOCKS and s % BLOCKS == 3
+                ready = u_units[s - 3 : s - 1]
+                for done in ready:
+                    turn_y(done)
+                if pair_run:
                     for i in range(2):
-                        turn_pairs(*groups[s // 4 - 1], i)
-                copy_y(u_units[s - 3])
-                if s >= BOTH_FROM:
-                    round_y(u_units[s - 3], True, True)
-                copy_y(u_units[s - 2])
-                if s >= SCALAR_ROUND_FROM:
-                    round_y(u_units[s - 2], True, True)
-                if s >= 7 and s % 4 == 3:
+                        turn_pairs(*groups[s // BLOCKS - 1], i)
+                for done in ready:
+                    copy_y(done)
+                    round_on_scalar(done)
+                if pair_run:
                     for i in range(2):
-                        copy_pairs(*groups[s // 4 - 1], i, True)
-                if s % 4 == 1:
-                    g, h = groups[s // 4 - 1]
-                    store_y(g, h, 0, TILES)
+                        copy_pairs(*groups[s // BLOCKS - 1], i, on_scalar)
+                g, j, h = ready[0]
+                store_y(g, h, j, j + 2)
 
-        last = u_units[12:]
-        u_product(last[2])
-        subtract(last[2])
-        weigh(last[2])
-        turn_y(last[0])
-        turn_y(last[1])
-        copy_y(last[0])
-        copy_y(last[1])
+        first, second, third, last = u_units[-BLOCKS:]
+        u_product(third)
+        subtract(third)
+        weigh(third)
+        turn_y(first)
+        turn_y(second)
+        copy_y(first)
+        copy_y(second)
         store_y(1, 1, 0, 2)
-        if TAIL == 1:
-            for i in range(2):
-                turn_pairs(1, 0, i)
-                copy_pairs(1, 0, i, True)
-        round_y(last[0], False, False)
-        u_product(last[3], 0, 2)
-        u_product(last[3], 2, 4)
-        subtract(last[3], 0, 2)
-        round_y(last[1], False, False)
-        weigh(last[3], 0, 2)
-        subtract(last[3], 2, 4)
-        turn_y(last[2])
-        round_y(last[2], True, True)
-        copy_y(last[2])
+        round_on_vector(first, y_tok[1, 1][:, :, 0:P])
+        u_product(last, 0, 2)
+        u_product(last, 2, 4)
+        subtract(last, 0, 2)
+        round_on_vector(second, y_tok[1, 1][:, :, P : 2 * P])
+        weigh(last, 0, 2)
+        subtract(last, 2, 4)
+        turn_y(third)
+        round_on_scalar(third)
+        copy_y(third)
         store_y(1, 1, 2, 3)
-        turn_y(last[3], 0, 2)
-        if TAIL == 1:
-            quantize_y(1, 0)
-        weigh(last[3], 2, 4)
-        round_y(last[3], False, True, 0, 2)
-        if TAIL == 0:
-            turn_pairs(1, 0, 0)
-        turn_y(last[3], 2, 4)
-        if TAIL == 0:
-            turn_pairs(1, 0, 1)
-        round_y(last[3], False, True, 2, 4)
-        if TAIL == 0:
-            copy_pairs(1, 0, 0, True)
-        copy_y(last[3], 0, 2)
-        copy_y(last[3], 2, 4)
+        turn_y(last, 0, 2)
+        weigh(last, 2, 4)
+        round_on_vector(last, y_turned[last, 0][:], 0, 2)
+        turn_pairs(1, 0, 0)
+        turn_y(last, 2, 4)
+        turn_pairs(1, 0, 1)
+        round_on_vector(last, y_turned[last, 2][:], 2, 4)
+        copy_pairs(1, 0, 0, on_scalar)
+        copy_y(last, 0, 2)
+        copy_y(last, 2, 4)
         store_y(1, 1, 3, 4)
         turn_pairs(1, 1, 0)
         turn_pairs(1, 1, 1)
-        if TAIL == 0:
-            copy_pairs(1, 0, 1, False)
-            copy_pairs(1, 1, 0, True)
-            quantize_y(1, 0)
-            copy_pairs(1, 1, 1, True)
-        else:
-            copy_pairs(1, 1, 0, False)
-            copy_pairs(1, 1, 1, True)
+        copy_pairs(1, 0, 1, on_vector)
+        copy_pairs(1, 1, 0, on_scalar)
+        quantize_y(1, 0)
+        copy_pairs(1, 1, 1, on_scalar)
         quantize_y(1, 1, 0, 2)
         quantize_y(1, 1, 2, 4)
         store_plane(1)

from contextlib import ExitStack

import concourse.mybir as mybir
from concourse.masks import make_identity

T, K, N = 1024, 2048, 1024
FLOPS = 2 * 2 * T * K * N

F32 = mybir.dt.float32
BF16 = mybir.dt.bfloat16
I32 = mybir.dt.int32
U32 = mybir.dt.uint32
U8 = mybir.dt.uint8
FP8 = mybir.dt.float8_e4m3fn
FP8X4 = mybir.dt.float8_e4m3fn_x4
FP4X4 = mybir.dt.float4_e2m1fn_x4
ACT = mybir.ActivationFunctionType
ALU = mybir.AluOpType

P = 128
PACK = 4
PASSES = K // (P * PACK)
HALF = 512
BLOCKS = HALF // P
QUADRANTS = 4
RUN = 4
LEAD = 12
JOBS_AFTER_UNIT = 2


def tile_distillation_curiosity_terms_b7_kernel(
    tc, x_words, x_scales, U_bytes, U_scale, R_words, R_scales, u_bias, r_bias, feat_weight, out_0, out_1, out_2
):
    nc = tc.nc
    on_vector, on_scalar = nc.vector.tensor_copy, nc.scalar.copy
    with ExitStack() as ctx:
        keep = ctx.enter_context(tc.tile_pool(name="keep", bufs=1))
        work = ctx.enter_context(tc.tile_pool(name="work", bufs=2))
        psum = ctx.enter_context(tc.psum_pool(name="psum", bufs=8))
        ctx.enter_context(tc.manual_schedule())

        x_plane = keep.tile([P, PASSES, T], U8, name="x_plane", align_bytes=64)
        r_plane = keep.tile([P, PASSES, N], U8, name="r_plane", align_bytes=64)
        nc.vector.memset(x_plane[:].rearrange("p c n -> p (c n)").bitcast(I32), 0)
        nc.vector.memset(r_plane[:].rearrange("p c n -> p (c n)").bitcast(I32), 0)

        scale_flat = keep.tile([P, 1], F32, name="scale_flat")
        nc.gpsimd.dma_start(out=scale_flat[:], in_=U_scale.rearrange("i (j o) -> (i j) o", o=1))
        ident = keep.tile([P, P], F32, name="ident")
        make_identity(nc, ident[:])
        vec_rows = keep.tile([P, P], BF16, name="vec_rows")
        nc.gpsimd.memset(vec_rows[:], 0.0)
        rows_per_vec = N // P

        u_raw, x_code, r_code = {}, {}, {}
        x_rows = x_words.rearrange("c p n t -> p c (n t)")
        r_rows = R_words.rearrange("c p b -> p c b")

        def load_u(c):
            u_raw[c] = keep.tile([P, PACK, N], U8, name="u_raw_%d" % c)
            rows = U_bytes[c * P * PACK : (c + 1) * P * PACK, :]
            nc.sync.dma_start(out=u_raw[c][:], in_=rows.rearrange("(p t) n -> p t n", t=PACK))

        def load_x(h, c0, c1):
            words = keep.tile([P, c1 - c0, HALF], U32, name="x_code_%d_%d" % (h, c0), align_bytes=64)
            src = x_rows[:, c0:c1, h * HALF * PACK : (h + 1) * HALF * PACK]
            nc.sync.dma_start(out=words[:].bitcast(I32), in_=src.bitcast(I32))
            for c in range(c0, c1):
                x_code[h, c] = words[:, c - c0, :]

        def load_r(g, c0, c1):
            words = keep.tile([P, c1 - c0, 2 * HALF], U8, name="r_code_%d_%d" % (g, c0), align_bytes=64)
            src = r_rows[:, c0:c1, g * HALF * 2 : (g + 1) * HALF * 2]
            nc.sync.dma_start(out=words[:].bitcast(I32), in_=src.bitcast(I32))
            for c in range(c0, c1):
                r_code[g, c] = words[:, c - c0, :]

        def load_plane(plane, scales, q0, q1):
            for q in range(q0, q1):
                src = scales[:, 4 * q : 4 * q + 4, :].rearrange("c r n -> r c n")
                nc.sync.dma_start(out=plane[32 * q : 32 * q + 4, :, :].bitcast(I32), in_=src.bitcast(I32))

        load_x(0, 0, 1)
        load_r(0, 0, 2)
        load_plane(x_plane, x_scales, 0, 1)
        load_u(0)
        load_plane(x_plane, x_scales, 1, QUADRANTS)
        load_plane(r_plane, R_scales, 0, QUADRANTS)
        load_x(0, 1, 2)
        load_x(0, 2, 3)
        load_r(0, 2, 4)
        for i, vec in enumerate((r_bias, u_bias, feat_weight)):
            rows = vec_rows[rows_per_vec * i : rows_per_vec * (i + 1), :]
            nc.sync.dma_start(out=rows, in_=vec.rearrange("o (j p) -> (o j) p", p=P))
        load_x(0, 3, 4)
        load_r(1, 0, 2)
        load_u(1)
        load_r(1, 2, 4)
        load_u(2)
        load_x(1, 0, 2)
        load_u(3)
        load_x(1, 2, 4)

        u_wide, u_grp, u_code, u_plane = {}, {}, {}, {}
        scale_col = keep.tile([P, PASSES, N // P], F32, name="scale_col")
        vec_col = keep.tile([P, 3 * rows_per_vec], F32, name="vec_col")

        def widen(g, c, t0, t1, copy):
            if t0 == 0:
                u_wide[g, c] = keep.tile([P, PACK, HALF], BF16, name="u_wide_%d_%d" % (g, c))
            for t in range(t0, t1):
                copy(out=u_wide[g, c][:, t, :], in_=u_raw[c][:, t, g * HALF : (g + 1) * HALF].bitcast(FP8))

        def interleave(g, c, j):
            if j == 0:
                u_grp[g, c] = work.tile([P, BLOCKS, P, PACK], BF16, name="u_grp", bufs=3, align_bytes=64)
            nc.vector.tensor_scalar(
                out=u_grp[g, c][:, j, :, :].rearrange("p (a i) t -> p a t i", i=RUN),
                in0=u_wide[g, c][:, :, j * P : (j + 1) * P].rearrange("p t (a i) -> p a t i", i=RUN),
                scalar1=scale_col[:, c, g * BLOCKS + j : g * BLOCKS + j + 1],
                scalar2=None,
                op0=ALU.mult,
            )

        def quantize_u(g, c, j0=0, j1=BLOCKS):
            if j0 == 0:
                u_code[g, c] = keep.tile([P, BLOCKS, P], U32, name="u_code_%d_%d" % (g, c), align_bytes=64)
                u_plane[g, c] = keep.tile([P, BLOCKS, P], U8, name="u_plane_%d_%d" % (g, c), align_bytes=64)
            nc.vector.quantize_mx(
                out=u_code[g, c][:, j0:j1, :].rearrange("p j n -> p (j n)").bitcast(FP8X4),
                scales=u_plane[g, c][:, j0:j1, :].rearrange("p j n -> p (j n)"),
                in_=u_grp[g, c][:, j0:j1, :, :].rearrange("p j n t -> p (j n t)"),
            )

        r_bank, target, pred, diff, y_feat, y_turned = {}, {}, {}, {}, {}, {}
        y_tok, y_pairs, pairs_turned, y_grp = {}, {}, {}, {}
        y_plane = keep.tile([P, N // HALF, T], U8, name="y_plane", align_bytes=64)

        def mx_pass(acc, h, c, weights, weight_scales, b0, b1):
            nc.tensor.matmul_mx(
                out=acc[:],
                lhsT=weights,
                lhsT_scale=weight_scales,
                rhs=x_code[h, c][:, b0 * P : b1 * P].bitcast(FP8X4),
                rhs_scale=x_plane[:, c, h * HALF + b0 * P : h * HALF + b1 * P],
                start=(c == 0),
                stop=(c == PASSES - 1),
            )

        def column(i, unit):
            n = rows_per_vec * i + unit[0] * BLOCKS + unit[1]
            return vec_col[:, n : n + 1]

        def r_products(units, c0=0, c1=PASSES):
            if c0 == 0:
                for unit in units:
                    r_bank[unit] = psum.tile([P, HALF], F32, name="bank")
            for c in range(c0, c1):
                for g, j, h in units:
                    weights = r_code[g, c][:, 2 * j * P : 2 * (j + 1) * P].bitcast(FP4X4)
                    n0 = g * HALF + j * P
                    mx_pass(r_bank[g, j, h], h, c, weights, r_plane[:, c, n0 : n0 + P], 0, BLOCKS)

        def tanh(units):
            for unit in units:
                target[unit] = work.tile([P, HALF], F32, name="target", bufs=LEAD)
                nc.scalar.activation(out=target[unit][:], in_=r_bank[unit][:], func=ACT.Tanh, bias=column(0, unit))

        def u_product(unit, b0=0, b1=BLOCKS):
            g, j, h = unit
            pred[unit, b0] = psum.tile([P, (b1 - b0) * P], F32, name="bank")
            for c in range(PASSES):
                mx_pass(pred[unit, b0], h, c, u_code[g, c][:, j, :].bitcast(FP8X4), u_plane[g, c][:, j, :], b0, b1)

        def subtract(unit, b0=0, b1=BLOCKS):
            diff[unit, b0] = work.tile([P, (b1 - b0) * P], F32, name="diff")
            nc.vector.scalar_tensor_tensor(
                out=diff[unit, b0][:],
                in0=pred[unit, b0][:],
                scalar=column(1, unit),
                in1=target[unit][:, b0 * P : b1 * P],
                op0=ALU.add,
                op1=ALU.subtract,
            )

        def weigh(unit, b0=0, b1=BLOCKS):
            y_feat[unit, b0] = work.tile([P, (b1 - b0) * P], F32, name="y_feat", bufs=5)
            nc.vector.scalar_tensor_tensor(
                out=y_feat[unit, b0][:],
                in0=diff[unit, b0][:],
                scalar=column(2, unit),
                in1=diff[unit, b0][:],
                op0=ALU.mult,
                op1=ALU.mult,
            )

        def turn_y(unit, b0=0, b1=BLOCKS):
            y_turned[unit, b0] = psum.tile([P, b1 - b0, P], F32, name="bank")
            for b in range(b1 - b0):
                nc.tensor.transpose(y_turned[unit, b0][:, b, :], y_feat[unit, b0][:, b * P : (b + 1) * P], ident[:])

        def copy_y(unit, b0=0, b1=BLOCKS):
            g, j, h = unit
            if j == 0:
                y_tok[g, h] = work.tile([P, BLOCKS, HALF], F32, name="y_tok", bufs=3)
            nc.scalar.copy(out=y_tok[g, h][:, b0:b1, j * P : (j + 1) * P], in_=y_turned[unit, b0][:])

        def store_y(g, h, j0, j1):
            rows = out_0[h * HALF : (h + 1) * HALF, g * HALF + j0 * P : g * HALF + j1 * P]
            nc.sync.dma_start(out=rows.rearrange("(b p) n -> p b n", p=P), in_=y_tok[g, h][:, :, j0 * P : j1 * P])

        def pair_views(unit, src, b0, b1):
            g, j, h = unit
            if j == 0:
                y_pairs[g, h] = work.tile([P, BLOCKS, 2, P, 2], BF16, name="y_pairs")
            words = P // PACK
            dst = y_pairs[g, h][:, b0:b1, :, words * j : words * (j + 1), :]
            return dst, src.rearrange("p b (q u e) -> p b u q e", u=2, e=2)

        def round_on_scalar(unit):
            dst, src = pair_views(unit, y_turned[unit, 0][:], 0, BLOCKS)
            nc.scalar.copy(out=dst, in_=src)

        def round_on_vector(unit, src, b0=0, b1=BLOCKS):
            dst, src = pair_views(unit, src, b0, b1)
            nc.vector.tensor_copy(out=dst, in_=src)

        def turn_pairs(g, h, i):
            words = y_pairs[g, h][:, 2 * i : 2 * i + 2].rearrange("p b u q e -> p (b u q e)").bitcast(F32)
            pairs_turned[g, h, i] = psum.tile([P, 2, 2, P], F32, name="bank")
            for b in range(2):
                for u in range(2):
                    w0 = (2 * b + u) * P
                    nc.tensor.transpose(pairs_turned[g, h, i][:, b, u, :], words[:, w0 : w0 + P], ident[:])

        def copy_pairs(g, h, i, copy):
            if i == 0:
                y_grp[g, h] = work.tile([P, HALF * PACK], BF16, name="y_grp", align_bytes=64)
            words = y_grp[g, h][:].bitcast(F32).rearrange("p (i b r u) -> p i b r u", i=2, b=2, u=2)
            copy(out=words[:, i, :, :, :], in_=pairs_turned[g, h, i][:].rearrange("p b u r -> p b r u"))

        def quantize_y(g, h, b0=0, b1=BLOCKS):
            codes = work.tile([P, (b1 - b0) * P], U32, name="y_code", bufs=3, align_bytes=64)
            m0, m1 = h * HALF + b0 * P, h * HALF + b1 * P
            nc.vector.quantize_mx(
                out=codes[:].bitcast(FP8X4),
                scales=y_plane[:, g, m0:m1],
                in_=y_grp[g, h][:, b0 * P * PACK : b1 * P * PACK],
            )
            dst = out_1[g].rearrange("p m t -> p (m t)")[:, m0 * PACK : m1 * PACK]
            nc.sync.dma_start(out=dst.bitcast(I32), in_=codes[:].bitcast(I32))

        def store_plane(g):
            for q in range(QUADRANTS):
                src = y_plane[32 * q : 32 * q + 4, g, :]
                nc.sync.dma_start(out=out_2[g, 4 * q : 4 * q + 4, :].bitcast(I32), in_=src.bitcast(I32))

        r_units = [(g, j, h) for h in range(2) for g in range(2) for j in range(BLOCKS)]
        u_units = [(g, j, h) for g in range(2) for h in range(2) for j in range(BLOCKS)]
        groups = [(g, h) for g in range(2) for h in range(2)]

        spread = psum.tile([P, 2, P], F32, name="bank")
        nc.tensor.transpose(spread[:, 0, :], scale_flat[:].to_broadcast([P, P]), ident[:])
        by_quadrant = spread[:, 0, :].rearrange("p (c q j) -> p q c j", q=QUADRANTS, j=N // P)
        for q in range(QUADRANTS):
            rows = slice(32 * q, 32 * q + 32)
            nc.vector.tensor_copy(out=scale_col[rows, :, :], in_=by_quadrant[rows, q, :, :])

        last_pass = PASSES - 1
        r_products(r_units[0:4], 0, last_pass)
        vec_wide = keep.tile([P, P], F32, name="vec_wide")
        nc.gpsimd.tensor_copy(out=vec_wide[:], in_=vec_rows[:])
        nc.tensor.transpose(spread[:, 1, :], vec_wide[:], ident[:])
        r_products(r_units[0:4], last_pass, PASSES)

        widen(0, 0, 0, PACK, on_vector)
        widen(1, 0, 0, PACK, on_scalar)
        for j in range(BLOCKS):
            interleave(0, 0, j)
        interleave(1, 0, 0)
        quantize_u(0, 0)
        for j in range(1, BLOCKS):
            interleave(1, 0, j)
        quantize_u(1, 0)
        widen(0, 1, 0, PACK, on_vector)

        nc.scalar.copy(out=vec_col[:], in_=spread[:, 1, 0 : 3 * rows_per_vec])
        tanh(r_units[0:4])
        r_products(r_units[4:8])
        r_products(r_units[8:LEAD])

        for c in range(1, last_pass):
            for j in range(BLOCKS):
                interleave(0, c, j)
            widen(0, c + 1, 0, PACK - 1, on_vector)
            widen(0, c + 1, PACK - 1, PACK, on_scalar)
            quantize_u(0, c)
        interleave(0, last_pass, 0)
        interleave(0, last_pass, 1)
        quantize_u(0, last_pass, 0, 1)
        interleave(0, last_pass, 2)
        interleave(0, last_pass, 3)
        quantize_u(0, last_pass, 1, 2)
        quantize_u(0, last_pass, 2, BLOCKS)

        tanh(r_units[4:8])
        widen(1, 1, 0, PACK, on_scalar)
        tanh(r_units[8:10])
        widen(1, 2, 0, PACK, on_scalar)
        tanh(r_units[10:LEAD])
        widen(1, 3, 0, PACK, on_scalar)

        jobs = []
        for c in range(1, PASSES):
            jobs.append((interleave, c, 0))
            if c > 1:
                jobs.append((quantize_u, c - 1, 0))
            jobs.extend([(interleave, c, j) for j in range(1, BLOCKS)])
        jobs.append((quantize_u, last_pass, 0))

        def run_jobs(count):
            for job in jobs[:count]:
                job[0](1, job[1], job[2])
                jobs.remove(job)

        for s, unit in enumerate(u_units[:-2]):
            u_product(unit)
            subtract(unit)
            if s > 2 * BLOCKS and s % BLOCKS == 1:
                quantize_y(*groups[s // BLOCKS - 2])
                if groups[s // BLOCKS - 2] == (0, 1):
                    store_plane(0)
            else:
                run_jobs(1)
            weigh(unit)
            if s + LEAD < len(r_units):
                r_products(r_units[s + LEAD : s + LEAD + 1])
                tanh(r_units[s + LEAD : s + LEAD + 1])
            run_jobs(JOBS_AFTER_UNIT)
            if s >= 3 and s % 2 == 1:
                pair_run = s > BLOCKS and s % BLOCKS == 3
                ready = u_units[s - 3 : s - 1]
                for done in ready:
                    turn_y(done)
                if pair_run:
                    for i in range(2):
                        turn_pairs(*groups[s // BLOCKS - 1], i)
                for done in ready:
                    copy_y(done)
                    round_on_scalar(done)
                if pair_run:
                    for i in range(2):
                        copy_pairs(*groups[s // BLOCKS - 1], i, on_scalar)
                g, j, h = ready[0]
                store_y(g, h, j, j + 2)

        first, second, third, last = u_units[-BLOCKS:]
        u_product(third)
        subtract(third)
        weigh(third)
        turn_y(first)
        turn_y(second)
        copy_y(first)
        copy_y(second)
        store_y(1, 1, 0, 2)
        round_on_vector(first, y_tok[1, 1][:, :, 0:P])
        u_product(last, 0, 2)
        u_product(last, 2, 4)
        subtract(last, 0, 2)
        round_on_vector(second, y_tok[1, 1][:, :, P : 2 * P])
        weigh(last, 0, 2)
        subtract(last, 2, 4)
        turn_y(third)
        round_on_scalar(third)
        copy_y(third)
        store_y(1, 1, 2, 3)
        turn_y(last, 0, 2)
        weigh(last, 2, 4)
        round_on_vector(last, y_turned[last, 0][:], 0, 2)
        turn_pairs(1, 0, 0)
        turn_y(last, 2, 4)
        turn_pairs(1, 0, 1)
        round_on_vector(last, y_turned[last, 2][:], 2, 4)
        copy_pairs(1, 0, 0, on_scalar)
        copy_y(last, 0, 2)
        copy_y(last, 2, 4)
        store_y(1, 1, 3, 4)
        turn_pairs(1, 1, 0)
        turn_pairs(1, 1, 1)
        copy_pairs(1, 0, 1, on_vector)
        copy_pairs(1, 1, 0, on_scalar)
        quantize_y(1, 0)
        copy_pairs(1, 1, 1, on_scalar)
        quantize_y(1, 1, 0, 2)
        quantize_y(1, 1, 2, 4)
        store_plane(1)
